import numpy as np
import ml_dtypes


def mxq(x, axis, fmt="e4m3"):
    dtype, down = {"e4m3": (ml_dtypes.float8_e4m3fn, 7), "e5m2": (ml_dtypes.float8_e5m2, 14)}[fmt]
    v = np.moveaxis(np.asarray(x, np.float32).astype(ml_dtypes.bfloat16).astype(np.float64), axis, -1)
    blocks = v.reshape(v.shape[:-1] + (-1, 32))
    amax = np.abs(blocks).max(-1, keepdims=True)
    byte = np.maximum(np.where(amax > 0, np.frexp(amax)[1] - 1 + 127, 0) - down, 1)
    scale = np.exp2(byte - 127.0)
    codes = (blocks / scale).astype(np.float32).astype(dtype).astype(np.float64)
    return np.moveaxis((codes * scale).reshape(v.shape), -1, axis)


WIDE = False


def mx_kscale(k):
    if not WIDE:
        return np.ones(k)
    levels = np.array([10, -10, 5, -5, 0])
    if k % 512:
        return np.exp2(np.random.permutation(np.resize(levels, k // 32))).repeat(32)
    a = np.empty((k // 512, 16))
    for p in range(k // 512):
        a[p, :8] = np.random.permutation(np.resize(levels, 8))
        for g in range(8):
            far = levels[np.abs(levels - a[p, g]) >= 10]
            a[p, g + 8] = far[np.random.randint(len(far))]
    return np.exp2(a.ravel()).repeat(32)


def f64(x):
    return np.asarray(x).astype(np.float64)


def striped(idx):
    return np.tile(idx.reshape(-1, 16).T, (8, 1)).astype(np.uint16)


def unstriped(offs):
    return offs[:16].T.reshape(-1).astype(np.int64)


E2M1 = np.array([0.0, 0.5, 1.0, 1.5, 2.0, 3.0, 4.0, 6.0, -0.0, -0.5, -1.0, -1.5, -2.0, -3.0, -4.0, -6.0])


def pack_weight(w, fmt):
    k, n = w.shape
    w = f64(np.asarray(w, np.float32).astype(ml_dtypes.bfloat16)).reshape(k // 32, 32, n)
    amax = np.abs(w).max(1)
    if fmt == "e4m3":
        byte = np.frexp(amax)[1] - 1 + 127 - 7
    else:
        mant, ex = np.frexp(amax / 6.0)
        byte = np.where(mant > 0.5, ex, ex - 1) + 127
    byte = np.clip(np.where(amax > 0, byte, 1), 1, 254)
    scaled = (w * np.exp2(127.0 - byte)[:, None, :]).reshape(k, n).astype(np.float32)
    by_word = np.ascontiguousarray(scaled.reshape(k // 512, 128, 4, n).transpose(0, 1, 3, 2))
    if fmt == "e4m3":
        words = by_word.astype(ml_dtypes.float8_e4m3fn).view(np.uint8)
    else:
        c = by_word.astype(ml_dtypes.float4_e2m1fn).view(np.uint8) & 0xF
        words = (c[..., 0::2] | (c[..., 1::2] << 4)).reshape(k // 512, 128, 2 * n)
    return np.ascontiguousarray(words), np.ascontiguousarray(byte.astype(np.uint8).reshape(k // 512, 16, n))


def unpack_weight(words, scales, fmt):
    g, _, n = scales.shape
    words = np.ascontiguousarray(words).reshape(g, 128, n, -1)
    if fmt == "e4m3":
        vals = words.view(ml_dtypes.float8_e4m3fn).astype(np.float64)
    else:
        nib = np.empty((g, 128, n, 4), np.uint8)
        nib[..., 0::2] = words & 0xF
        nib[..., 1::2] = words >> 4
        vals = E2M1[nib]
    vals = vals * np.repeat(np.exp2(scales.astype(np.float64) - 127.0), 8, axis=1)[..., None]
    return vals.transpose(0, 1, 3, 2).reshape(g * 512, n)


def gelu(v):
    return 0.5 * v * (1.0 + np.tanh(np.sqrt(2.0 / np.pi) * (v + 0.044715 * v**3)))


K, T, S, T2, H, N = 1024, 4096, 1024, 2048, 512, 256

def setup_inputs():
    n = np.random.standard_normal
    s = mx_kscale(K)[:, None]
    u = mx_kscale(H)[:, None]
    tab_words, tab_scales = pack_weight(n((K, T)) * s, "e4m3")
    wa_words, wa_scales = pack_weight(n((K, H)) / np.sqrt(K) / s * u.T, "e2m1")
    return {
        "tab_words": tab_words, "tab_scales": tab_scales,
        "offs": striped(np.random.permutation(T)[:S]),
        "wa_words": wa_words, "wa_scales": wa_scales,
        "wg": (n((K, H)) / np.sqrt(K) / s).astype(np.float32),
        "wgs": np.exp(0.3 * n((128, S))).astype(np.float32),
        "offs2": striped(np.random.permutation(T2)[:S]),
        "sites": (n((H, T2)) * u).astype(np.float32),
        "wo": (n((H, N)) / np.sqrt(H) / u).astype(np.float32),
    }

def reference(tab_words, tab_scales, offs, wa_words, wa_scales, wg, wgs, offs2, sites, wo):
    v = unpack_weight(tab_words, tab_scales, "e4m3")[:, unstriped(offs)]
    wa = unpack_weight(wa_words, wa_scales, "e2m1")
    a = wa.T @ v
    b = mxq(f64(wg), 0, "e4m3").T @ v
    h = a * np.exp(-np.square(b))
    page = np.zeros((H, T2))
    page[:, unstriped(offs2)] = np.tile(f64(wgs), (H // 128, 1)) * h
    z = page + f64(sites)
    return mxq(f64(wo), 0, "e4m3").T @ mxq(z, 0, "e4m3")

@@ -1,0 +1,290 @@
+from contextlib import ExitStack
+
+import concourse.mybir as mybir
+from concourse.masks import make_identity
+
+K, T, S, T2, H, N = 1024, 4096, 1024, 2048, 512, 256
+FLOPS = 2 * (2 * K * H * S + H * N * T2)
+
+F32 = mybir.dt.float32
+BF16 = mybir.dt.bfloat16
+I32 = mybir.dt.int32
+U32 = mybir.dt.uint32
+U16 = mybir.dt.uint16
+U8 = mybir.dt.uint8
+FP8X4 = mybir.dt.float8_e4m3fn_x4
+FP4X4 = mybir.dt.float4_e2m1fn_x4
+ACT = mybir.ActivationFunctionType
+MULT = mybir.AluOpType.mult
+
+P = 128
+PACK = 4
+PASSES = K // (P * PACK)
+BANK = 512
+HALVES = S // BANK
+ROWS = H // P
+GROUPS = T2 // BANK
+CHUNKS = BANK // P
+COLS = BANK // 16
+
+
+def tile_list_gaussian_atom_sites_kernel(
+    tc, tab_words, tab_scales, offs, wa_words, wa_scales, wg, wgs, offs2, sites, wo, out
+):
+    nc = tc.nc
+    with ExitStack() as ctx:
+        lists = ctx.enter_context(tc.tile_pool(name="lists", bufs=1))
+        keep = ctx.enter_context(tc.tile_pool(name="keep", bufs=1))
+        ring = ctx.enter_context(tc.tile_pool(name="ring", bufs=3))
+        psum = ctx.enter_context(tc.psum_pool(name="psum", bufs=1))
+
+        banks = [psum.tile([P, BANK], F32, name=f"bank{b}") for b in range(8)]
+
+        atoms = lists.tile([P, S // 16], U16, name="atoms")
+        places = lists.tile([P, S // 16], U16, name="places")
+        table_words = [keep.tile([P, T], I32, name=f"table_words{a}") for a in range(PASSES)]
+        table_scales = keep.tile(
+            [P, PASSES, T // 4], I32, name="table_scales", tag="scales_then_codes", align_bytes=64
+        )
+        wa_codes = keep.tile([P, PASSES, 2 * H // 4], I32, name="wa_codes", align_bytes=64)
+        wa_plane = keep.tile([P, PASSES, H // 4], I32, name="wa_plane", align_bytes=64)
+        wg_first = [keep.tile([P, PACK, P], F32, name=f"wg_first{a}") for a in range(PASSES)]
+        wg_rest = [keep.tile([P, PACK, H - P], F32, name=f"wg_rest{a}") for a in range(PASSES)]
+        weights = [keep.tile([P, BANK], F32, name=f"weights{h}") for h in range(HALVES)]
+        states = [keep.tile([P, T2], F32, name=f"states{i}") for i in range(ROWS)]
+        pages = [keep.tile([P, T2], F32, name=f"pages{i}") for i in range(ROWS)]
+        wo_raw = keep.tile([P, PACK, N], F32, name="wo_raw")
+        identity = keep.tile([P, P], F32, name="identity")
+        warm = keep.tile([P, 8], F32, name="warm")
+
+        nc.vector.memset(table_scales[:], 0)
+        nc.gpsimd.memset(wa_plane[:], 0)
+        nc.gpsimd.memset(warm[:], 0.0)
+        make_identity(nc, identity[:])
+        nc.scalar.activation(warm[:], warm[:], ACT.Exp)
+        for r in range(4):
+            nc.gpsimd.dma_start(
+                table_scales[r:P:32, :, :],
+                tab_scales[:, r:16:4, :].rearrange("a q t -> q a t").bitcast(I32),
+            )
+        for r in range(4):
+            nc.gpsimd.dma_start(
+                wa_plane[r:P:32, :, :],
+                wa_scales[:, r:16:4, :].rearrange("a q c -> q a c").bitcast(I32),
+            )
+        for page in pages:
+            nc.gpsimd.memset(page[:], 0.0)
+
+        def wg_rows(a):
+            return wg[a * P * PACK : (a + 1) * P * PACK, :].rearrange("(p i) r -> p i r", i=PACK)
+
+        def load_words(a):
+            nc.sync.dma_start(
+                table_words[a][:], tab_words[a].rearrange("p t i -> p (t i)").bitcast(I32)
+            )
+
+        nc.sync.dma_start(atoms[:], offs)
+        load_words(0)
+        nc.sync.dma_start(wa_codes[:], wa_words.rearrange("a p b -> p a b").bitcast(I32))
+        for a in range(PASSES):
+            nc.sync.dma_start(wg_first[a][:], wg_rows(a)[:, :, :P])
+        load_words(1)
+        nc.sync.dma_start(weights[0][:], wgs[:, :BANK])
+        nc.sync.dma_start(places[:], offs2)
+        nc.sync.dma_start(weights[1][:], wgs[:, BANK:])
+        for a in range(PASSES):
+            nc.sync.dma_start(wg_rest[a][:], wg_rows(a)[:, :, P:])
+        nc.sync.dma_start(states[0][:], sites[:P, :])
+        nc.sync.dma_start(wo_raw[:], wo.rearrange("(p i) n -> p i n", i=PACK))
+        for i in range(1, ROWS):
+            nc.sync.dma_start(states[i][:], sites[i * P : (i + 1) * P, :])
+
+        v_codes, v_plane = {}, {}
+
+        def gather_scales(a, h):
+            v_plane[a, h] = keep.tile([P, BANK], U8, name=f"v_plane{a}{h}", align_bytes=64)
+            nc.vector.tensor_copy(
+                v_plane[a, h][:],
+                table_scales[:, a, :].bitcast(U8).indirect(atoms[:, h * COLS : (h + 1) * COLS]),
+            )
+
+        def gather_words(a, h, picked):
+            v_codes[a, h] = picked[:, h * BANK : (h + 1) * BANK]
+            nc.vector.tensor_copy(
+                v_codes[a, h],
+                table_words[a][:].bitcast(U32).indirect(atoms[:, h * COLS : (h + 1) * COLS]),
+            )
+
+        def quantize(grouped, width, name):
+            codes = keep.tile([P, width], U32, name=f"{name}_codes", align_bytes=64)
+            plane = keep.tile([P, width], U8, name=f"{name}_plane", align_bytes=64)
+            nc.vector.quantize_mx(out=codes[:].bitcast(FP8X4), scales=plane[:], in_=grouped)
+            return codes, plane
+
+        wg_q = {}
+
+        def quantize_wg(i):
+            grouped = keep.tile([P, PASSES, P, PACK], BF16, name=f"wg_grouped{i}", align_bytes=64)
+            for a in range(PASSES):
+                raw = wg_first[a][:] if i == 0 else wg_rest[a][:, :, (i - 1) * P : i * P]
+                nc.scalar.copy(grouped[:, a, :, :], raw.rearrange("p i r -> p r i"))
+            wg_q[i] = quantize(
+                grouped[:].rearrange("p a r i -> p (a r i)"), PASSES * P, f"wg{i}"
+            )
+
+        for h in range(HALVES):
+            for a in range(PASSES):
+                gather_scales(a, h)
+        picked_first = keep.tile([P, S], U32, name="picked_first", align_bytes=64)
+        for h in range(HALVES):
+            gather_words(0, h, picked_first)
+        quantize_wg(0)
+        picked_second = keep.tile(
+            [P, S], U32, name="picked_second", tag="scales_then_codes", align_bytes=64
+        )
+        for h in range(HALVES):
+            gather_words(1, h, picked_second)
+
+        gate, weighted, message = {}, {}, {}
+
+        def products(k):
+            i, h = divmod(k, HALVES)
+            a_bank, b_bank = banks[2 * (k % 2)], banks[2 * (k % 2) + 1]
+            wg_codes, wg_plane = wg_q[i]
+            for a in range(PASSES):
+                nc.tensor.matmul_mx(
+                    out=b_bank[:],
+                    lhsT=wg_codes[:, a * P : (a + 1) * P].bitcast(FP8X4),
+                    lhsT_scale=wg_plane[:, a * P : (a + 1) * P],
+                    rhs=v_codes[a, h].bitcast(FP8X4),
+                    rhs_scale=v_plane[a, h][:],
+                    start=(a == 0),
+                    stop=(a == PASSES - 1),
+                )
+            for a in range(PASSES):
+                nc.tensor.matmul_mx(
+                    out=a_bank[:],
+                    lhsT=wa_codes[:, a, :].bitcast(U8)[:, 2 * i * P : 2 * (i + 1) * P].bitcast(FP4X4),
+                    lhsT_scale=wa_plane[:, a, :].bitcast(U8)[:, i * P : (i + 1) * P],
+                    rhs=v_codes[a, h].bitcast(FP8X4),
+                    rhs_scale=v_plane[a, h][:],
+                    start=(a == 0),
+                    stop=(a == PASSES - 1),
+                )
+            square = ring.tile([P, BANK], F32, name="square")
+            nc.scalar.activation(square[:], b_bank[:], ACT.Square)
+            gate[k] = ring.tile([P, BANK], F32, name="gate")
+            nc.scalar.activation(gate[k][:], square[:], ACT.Exp, scale=-1.0)
+            weighted[k] = ring.tile([P, BANK], F32, name="weighted")
+            nc.vector.tensor_tensor(weighted[k][:], a_bank[:], weights[h][:], MULT)
+
+        def gate_message(k):
+            message[k] = ring.tile([P, BANK], F32, name="message")
+            nc.vector.tensor_tensor(message[k][:], weighted[k][:], gate[k][:], MULT)
+
+        def scatter(k):
+            i, h = divmod(k, HALVES)
+            nc.vector.tensor_copy(
+                pages[i][:].indirect(places[:, h * COLS : (h + 1) * COLS]), message[k][:]
+            )
+
+        def turn(source, first):
+            for g in range(GROUPS):
+                for c in range(CHUNKS):
+                    t0 = g * BANK + c * P
+                    nc.tensor.matmul(
+                        banks[4 + g][:, c * P : (c + 1) * P],
+                        lhsT=source[:, t0 : t0 + P],
+                        rhs=identity[:],
+                        is_transpose=True,
+                        start=(first and c == 0),
+                        stop=(not first and c == CHUNKS - 1),
+                    )
+
+        z_rows = [keep.tile([P, 2, CHUNKS, 2 * P], BF16, name=f"z_rows{g}") for g in range(GROUPS)]
+
+        def copy_on(engine, dst, src):
+            if engine == "vector":
+                nc.vector.tensor_copy(dst, src)
+            else:
+                nc.scalar.copy(dst, src)
+
+        def round_z(i, g, engine):
+            copy_on(
+                engine,
+                z_rows[g][:, :, :, 64 * i : 64 * (i + 1)].rearrange("p u c (m e) -> p u c m e", e=2),
+                banks[4 + g][:].rearrange("p (c m u e) -> p u c m e", c=CHUNKS, u=2, e=2),
+            )
+
+        units = ROWS * HALVES
+        wo_q = []
+        products(0)
+        gate_message(0)
+        products(1)
+        for k in range(units):
+            i, h = divmod(k, HALVES)
+            if h == 0:
+                turn(states[i], True)
+                if i + 1 < ROWS:
+                    quantize_wg(i + 1)
+                else:
+                    wo_grouped = keep.tile([P, N, PACK], BF16, name="wo_grouped", align_bytes=64)
+                    nc.scalar.copy(wo_grouped[:], wo_raw[:].rearrange("p i n -> p n i"))
+                    wo_q.extend(quantize(wo_grouped[:].rearrange("p n i -> p (n i)"), N, "wo"))
+            scatter(k)
+            if k + 1 < units:
+                gate_message(k + 1)
+            if k + 2 < units:
+                products(k + 2)
+            if h == HALVES - 1:
+                turn(pages[i], False)
+                for g in range(GROUPS):
+                    round_z(i, g, "vector" if i == ROWS - 1 and g % 2 == 0 else "scalar")
+
+        wo_codes, wo_plane = wo_q
+        z_grouped = {}
+
+        def turn_back(g):
+            z_grouped[g] = ring.tile([P, BANK, PACK], BF16, name="z_grouped", align_bytes=64)
+            words = z_rows[g][:].bitcast(F32)
+            grouped_words = z_grouped[g][:].rearrange("p t i -> p (t i)").bitcast(F32)
+            for half in range(2):
+                bank = banks[2 * (g % 2) + half]
+                for c2 in range(2):
+                    for u in range(2):
+                        col = (2 * c2 + u) * P
+                        nc.tensor.transpose(
+                            bank[:, col : col + P], words[:, u, 2 * half + c2, :], identity[:]
+                        )
+                copy_on(
+                    "scalar" if half == 0 else "vector",
+                    grouped_words[:, half * BANK : (half + 1) * BANK].rearrange(
+                        "p (c t u) -> p c t u", c=2, u=2
+                    ),
+                    bank[:].rearrange("p (c u t) -> p c t u", c=2, u=2),
+                )
+
+        def project(g):
+            z_codes, z_plane = quantize(
+                z_grouped[g][:].rearrange("p t i -> p (t i)"), BANK, f"z{g}"
+            )
+            for n in range(N // P):
+                bank = banks[4 + 2 * (g % 2) + n]
+                nc.tensor.matmul_mx(
+                    out=bank[:],
+                    lhsT=wo_codes[:, n * P : (n + 1) * P].bitcast(FP8X4),
+                    lhsT_scale=wo_plane[:, n * P : (n + 1) * P],
+                    rhs=z_codes[:].bitcast(FP8X4),
+                    rhs_scale=z_plane[:],
+                    start=True,
+                    stop=True,
+                )
+                result = keep.tile([P, BANK], F32, name=f"result{g}{n}")
+                copy_on("vector" if n == 1 and g >= 2 else "scalar", result[:], bank[:])
+                nc.sync.dma_start(out[n * P : (n + 1) * P, g * BANK : (g + 1) * BANK], result[:])
+
+        turn_back(0)
+        for g in range(GROUPS):
+            if g + 1 < GROUPS:
+                turn_back(g + 1)
+            project(g)

@@ -43,9 +43,7 @@ def tile_list_gaussian_atom_sites_kernel(
         atoms = lists.tile([P, S // 16], U16, name="atoms")
         places = lists.tile([P, S // 16], U16, name="places")
         table_words = [keep.tile([P, T], I32, name=f"table_words{a}") for a in range(PASSES)]
-        table_scales = keep.tile(
-            [P, PASSES, T // 4], I32, name="table_scales", tag="scales_then_codes", align_bytes=64
-        )
+        table_scales = keep.tile([P, PASSES, T // 4], I32, name="table_scales")
         wa_codes = keep.tile([P, PASSES, 2 * H // 4], I32, name="wa_codes", align_bytes=64)
         wa_plane = keep.tile([P, PASSES, H // 4], I32, name="wa_plane", align_bytes=64)
         wg_first = [keep.tile([P, PACK, P], F32, name=f"wg_first{a}") for a in range(PASSES)]
@@ -57,24 +55,6 @@ def tile_list_gaussian_atom_sites_kernel(
         identity = keep.tile([P, P], F32, name="identity")
         warm = keep.tile([P, 8], F32, name="warm")
 
-        nc.vector.memset(table_scales[:], 0)
-        nc.gpsimd.memset(wa_plane[:], 0)
-        nc.gpsimd.memset(warm[:], 0.0)
-        make_identity(nc, identity[:])
-        nc.scalar.activation(warm[:], warm[:], ACT.Exp)
-        for r in range(4):
-            nc.gpsimd.dma_start(
-                table_scales[r:P:32, :, :],
-                tab_scales[:, r:16:4, :].rearrange("a q t -> q a t").bitcast(I32),
-            )
-        for r in range(4):
-            nc.gpsimd.dma_start(
-                wa_plane[r:P:32, :, :],
-                wa_scales[:, r:16:4, :].rearrange("a q c -> q a c").bitcast(I32),
-            )
-        for page in pages:
-            nc.gpsimd.memset(page[:], 0.0)
-
         def wg_rows(a):
             return wg[a * P * PACK : (a + 1) * P * PACK, :].rearrange("(p i) r -> p i r", i=PACK)
 
@@ -83,17 +63,35 @@ def tile_list_gaussian_atom_sites_kernel(
                 table_words[a][:], tab_words[a].rearrange("p t i -> p (t i)").bitcast(I32)
             )
 
+        nc.vector.memset(table_scales[:], 0)
+        nc.gpsimd.memset(wa_plane[:], 0)
+        nc.gpsimd.memset(warm[:], 0.0)
+        nc.scalar.activation(warm[:], warm[:], ACT.Exp)
+        for r in range(4):
+            nc.gpsimd.dma_start(
+                wa_plane[r:P:32, :, :],
+                wa_scales[:, r:16:4, :].rearrange("a q c -> q a c").bitcast(I32),
+            )
+        make_identity(nc, identity[:])
+        for i in range(ROWS):
+            (nc.vector if i < 2 else nc.gpsimd).memset(pages[i][:], 0.0)
+
         nc.sync.dma_start(atoms[:], offs)
+        nc.sync.dma_start(places[:], offs2)
         load_words(0)
-        nc.sync.dma_start(wa_codes[:], wa_words.rearrange("a p b -> p a b").bitcast(I32))
+        for r in range(4):
+            nc.sync.dma_start(
+                table_scales[r:P:32, :, :],
+                tab_scales[:, r:16:4, :].rearrange("a q t -> q a t").bitcast(I32),
+            )
         for a in range(PASSES):
             nc.sync.dma_start(wg_first[a][:], wg_rows(a)[:, :, :P])
+        nc.sync.dma_start(wa_codes[:], wa_words.rearrange("a p b -> p a b").bitcast(I32))
         load_words(1)
         nc.sync.dma_start(weights[0][:], wgs[:, :BANK])
-        nc.sync.dma_start(places[:], offs2)
-        nc.sync.dma_start(weights[1][:], wgs[:, BANK:])
         for a in range(PASSES):
             nc.sync.dma_start(wg_rest[a][:], wg_rows(a)[:, :, P:])
+        nc.sync.dma_start(weights[1][:], wgs[:, BANK:])
         nc.sync.dma_start(states[0][:], sites[:P, :])
         nc.sync.dma_start(wo_raw[:], wo.rearrange("(p i) n -> p i n", i=PACK))
         for i in range(1, ROWS):
@@ -109,7 +107,7 @@ def tile_list_gaussian_atom_sites_kernel(
             )
 
         def gather_words(a, h, picked):
-            v_codes[a, h] = picked[:, h * BANK : (h + 1) * BANK]
+            v_codes[a, h] = picked[:, a, h * BANK : (h + 1) * BANK]
             nc.vector.tensor_copy(
                 v_codes[a, h],
                 table_words[a][:].bitcast(U32).indirect(atoms[:, h * COLS : (h + 1) * COLS]),
@@ -123,44 +121,46 @@ def tile_list_gaussian_atom_sites_kernel(
 
         wg_q = {}
 
-        def quantize_wg(i):
+        def quantize_wg(i, raw):
             grouped = keep.tile([P, PASSES, P, PACK], BF16, name=f"wg_grouped{i}", align_bytes=64)
             for a in range(PASSES):
-                raw = wg_first[a][:] if i == 0 else wg_rest[a][:, :, (i - 1) * P : i * P]
-                nc.scalar.copy(grouped[:, a, :, :], raw.rearrange("p i r -> p r i"))
+                nc.scalar.copy(grouped[:, a, :, :], raw[a].rearrange("p i r -> p r i"))
             wg_q[i] = quantize(
                 grouped[:].rearrange("p a r i -> p (a r i)"), PASSES * P, f"wg{i}"
             )
 
+        picked = keep.tile([P, PASSES, S], U32, name="picked", align_bytes=64)
+        for h in range(HALVES):
+            gather_words(0, h, picked)
         for h in range(HALVES):
             for a in range(PASSES):
                 gather_scales(a, h)
-        picked_first = keep.tile([P, S], U32, name="picked_first", align_bytes=64)
+        quantize_wg(0, [wg_first[a][:] for a in range(PASSES)])
         for h in range(HALVES):
-            gather_words(0, h, picked_first)
-        quantize_wg(0)
-        picked_second = keep.tile(
-            [P, S], U32, name="picked_second", tag="scales_then_codes", align_bytes=64
-        )
-        for h in range(HALVES):
-            gather_words(1, h, picked_second)
+            gather_words(1, h, picked)
 
-        gate, weighted, message = {}, {}, {}
+        gate, weighted = {}, {}
 
-        def products(k):
-            i, h = divmod(k, HALVES)
-            a_bank, b_bank = banks[2 * (k % 2)], banks[2 * (k % 2) + 1]
+        def gate_product(i, h, bank, start, stop, a):
             wg_codes, wg_plane = wg_q[i]
+            nc.tensor.matmul_mx(
+                out=bank[:],
+                lhsT=wg_codes[:, a * P : (a + 1) * P].bitcast(FP8X4),
+                lhsT_scale=wg_plane[:, a * P : (a + 1) * P],
+                rhs=v_codes[a, h].bitcast(FP8X4),
+                rhs_scale=v_plane[a, h][:],
+                start=start,
+                stop=stop,
+            )
+
+        def products(i, h):
+            cols = slice(h * BANK, (h + 1) * BANK)
+            a_bank, b_bank = banks[2 * h], banks[2 * h + 1]
+            if h == 0:
+                gate[i] = ring.tile([P, S], F32, name="gate", bufs=2)
+                weighted[i] = ring.tile([P, S], F32, name="weighted", bufs=2)
             for a in range(PASSES):
-                nc.tensor.matmul_mx(
-                    out=b_bank[:],
-                    lhsT=wg_codes[:, a * P : (a + 1) * P].bitcast(FP8X4),
-                    lhsT_scale=wg_plane[:, a * P : (a + 1) * P],
-                    rhs=v_codes[a, h].bitcast(FP8X4),
-                    rhs_scale=v_plane[a, h][:],
-                    start=(a == 0),
-                    stop=(a == PASSES - 1),
-                )
+                gate_product(i, h, b_bank, a == 0, a == PASSES - 1, a)
             for a in range(PASSES):
                 nc.tensor.matmul_mx(
                     out=a_bank[:],
@@ -171,29 +171,32 @@ def tile_list_gaussian_atom_sites_kernel(
                     start=(a == 0),
                     stop=(a == PASSES - 1),
                 )
-            square = ring.tile([P, BANK], F32, name="square")
+            square = ring.tile([P, BANK], F32, name="square", bufs=2)
             nc.scalar.activation(square[:], b_bank[:], ACT.Square)
-            gate[k] = ring.tile([P, BANK], F32, name="gate")
-            nc.scalar.activation(gate[k][:], square[:], ACT.Exp, scale=-1.0)
-            weighted[k] = ring.tile([P, BANK], F32, name="weighted")
-            nc.vector.tensor_tensor(weighted[k][:], a_bank[:], weights[h][:], MULT)
+            nc.scalar.activation(gate[i][:, cols], square[:], ACT.Exp, scale=-1.0)
 
-        def gate_message(k):
-            message[k] = ring.tile([P, BANK], F32, name="message")
-            nc.vector.tensor_tensor(message[k][:], weighted[k][:], gate[k][:], MULT)
+        def weigh(i, h):
+            cols = slice(h * BANK, (h + 1) * BANK)
+            nc.vector.tensor_tensor(weighted[i][:, cols], banks[2 * h][:], weights[h][:], MULT)
 
-        def scatter(k):
-            i, h = divmod(k, HALVES)
-            nc.vector.tensor_copy(
-                pages[i][:].indirect(places[:, h * COLS : (h + 1) * COLS]), message[k][:]
+        def scatter(i, first, last):
+            cols = slice(first * BANK, last * BANK)
+            nc.vector.tensor_tensor(
+                pages[i][:].indirect(places[:, first * COLS : last * COLS]),
+                weighted[i][:, cols],
+                gate[i][:, cols],
+                MULT,
             )
 
-        def turn(source, first):
+        early_banks = banks[4:]
+        late_banks = [banks[1], banks[3], banks[0], banks[2]]
+
+        def turn(source, first, into):
             for g in range(GROUPS):
                 for c in range(CHUNKS):
                     t0 = g * BANK + c * P
                     nc.tensor.matmul(
-                        banks[4 + g][:, c * P : (c + 1) * P],
+                        into[g][:, c * P : (c + 1) * P],
                         lhsT=source[:, t0 : t0 + P],
                         rhs=identity[:],
                         is_transpose=True,
@@ -209,39 +212,49 @@ def tile_list_gaussian_atom_sites_kernel(
             else:
                 nc.scalar.copy(dst, src)
 
-        def round_z(i, g, engine):
+        def round_z(i, g, engine, into):
             copy_on(
                 engine,
                 z_rows[g][:, :, :, 64 * i : 64 * (i + 1)].rearrange("p u c (m e) -> p u c m e", e=2),
-                banks[4 + g][:].rearrange("p (c m u e) -> p u c m e", c=CHUNKS, u=2, e=2),
+                into[g][:].rearrange("p (c m u e) -> p u c m e", c=CHUNKS, u=2, e=2),
             )
 
-        units = ROWS * HALVES
-        wo_q = []
-        products(0)
-        gate_message(0)
-        products(1)
-        for k in range(units):
-            i, h = divmod(k, HALVES)
-            if h == 0:
-                turn(states[i], True)
-                if i + 1 < ROWS:
-                    quantize_wg(i + 1)
-                else:
-                    wo_grouped = keep.tile([P, N, PACK], BF16, name="wo_grouped", align_bytes=64)
-                    nc.scalar.copy(wo_grouped[:], wo_raw[:].rearrange("p i n -> p n i"))
-                    wo_q.extend(quantize(wo_grouped[:].rearrange("p n i -> p (n i)"), N, "wo"))
-            scatter(k)
-            if k + 1 < units:
-                gate_message(k + 1)
-            if k + 2 < units:
-                products(k + 2)
-            if h == HALVES - 1:
-                turn(pages[i], False)
-                for g in range(GROUPS):
-                    round_z(i, g, "vector" if i == ROWS - 1 and g % 2 == 0 else "scalar")
+        def next_wg(i):
+            quantize_wg(i, [wg_rest[a][:, :, (i - 1) * P : i * P] for a in range(PASSES)])
 
-        wo_codes, wo_plane = wo_q
+        last = ROWS - 1
+        for h in range(HALVES):
+            products(0, h)
+        for i in range(ROWS):
+            if i == 0:
+                weigh(i, 0)
+                scatter(i, 0, 1)
+                weigh(i, 1)
+                next_wg(i + 1)
+                scatter(i, 1, 2)
+            elif i < last:
+                weigh(i, 0)
+                weigh(i, 1)
+                next_wg(i + 1)
+                scatter(i, 0, 2)
+            else:
+                weigh(i, 0)
+                weigh(i, 1)
+                wo_grouped = keep.tile([P, N, PACK], BF16, name="wo_grouped", align_bytes=64)
+                nc.scalar.copy(wo_grouped[:], wo_raw[:].rearrange("p i n -> p n i"))
+                wo_codes, wo_plane = quantize(
+                    wo_grouped[:].rearrange("p n i -> p (n i)"), N, "wo"
+                )
+                scatter(i, 0, 2)
+            if i < last:
+                for h in range(HALVES):
+                    products(i + 1, h)
+            into = late_banks if i == last else early_banks
+            turn(states[i][:], True, into)
+            turn(pages[i][:], False, into)
+            for g in range(GROUPS):
+                round_z(i, g, "vector" if i == last and g % 2 == 0 else "scalar", into)
+
         z_grouped = {}
 
         def turn_back(g):
@@ -249,7 +262,7 @@ def tile_list_gaussian_atom_sites_kernel(
             words = z_rows[g][:].bitcast(F32)
             grouped_words = z_grouped[g][:].rearrange("p t i -> p (t i)").bitcast(F32)
             for half in range(2):
-                bank = banks[2 * (g % 2) + half]
+                bank = early_banks[2 * (g % 2) + half]
                 for c2 in range(2):
                     for u in range(2):
                         col = (2 * c2 + u) * P
@@ -269,7 +282,7 @@ def tile_list_gaussian_atom_sites_kernel(
                 z_grouped[g][:].rearrange("p t i -> p (t i)"), BANK, f"z{g}"
             )
             for n in range(N // P):
-                bank = banks[4 + 2 * (g % 2) + n]
+                bank = late_banks[2 * (g % 2) + n]
                 nc.tensor.matmul_mx(
                     out=bank[:],
                     lhsT=wo_codes[:, n * P : (n + 1) * P].bitcast(FP8X4),

@@ -47,7 +47,10 @@ def tile_list_gaussian_atom_sites_kernel(
         wa_codes = keep.tile([P, PASSES, 2 * H // 4], I32, name="wa_codes", align_bytes=64)
         wa_plane = keep.tile([P, PASSES, H // 4], I32, name="wa_plane", align_bytes=64)
         wg_first = [keep.tile([P, PACK, P], F32, name=f"wg_first{a}") for a in range(PASSES)]
-        wg_rest = [keep.tile([P, PACK, H - P], F32, name=f"wg_rest{a}") for a in range(PASSES)]
+        wg_rest = [
+            keep.tile([P, PACK, H - P], F32, name=f"wg_rest{a}", tag=f"spent{a}", align_bytes=64)
+            for a in range(PASSES)
+        ]
         weights = [keep.tile([P, BANK], F32, name=f"weights{h}") for h in range(HALVES)]
         states = [keep.tile([P, T2], F32, name=f"states{i}") for i in range(ROWS)]
         pages = [keep.tile([P, T2], F32, name=f"pages{i}") for i in range(ROWS)]
@@ -86,8 +89,8 @@ def tile_list_gaussian_atom_sites_kernel(
             )
         for a in range(PASSES):
             nc.sync.dma_start(wg_first[a][:], wg_rows(a)[:, :, :P])
-        nc.sync.dma_start(wa_codes[:], wa_words.rearrange("a p b -> p a b").bitcast(I32))
         load_words(1)
+        nc.sync.dma_start(wa_codes[:], wa_words.rearrange("a p b -> p a b").bitcast(I32))
         nc.sync.dma_start(weights[0][:], wgs[:, :BANK])
         for a in range(PASSES):
             nc.sync.dma_start(wg_rest[a][:], wg_rows(a)[:, :, P:])
@@ -113,8 +116,10 @@ def tile_list_gaussian_atom_sites_kernel(
                 table_words[a][:].bitcast(U32).indirect(atoms[:, h * COLS : (h + 1) * COLS]),
             )
 
-        def quantize(grouped, width, name):
-            codes = keep.tile([P, width], U32, name=f"{name}_codes", align_bytes=64)
+        def quantize(grouped, width, name, tag=None):
+            codes = keep.tile(
+                [P, width], U32, name=f"{name}_codes", tag=tag or f"{name}_codes", align_bytes=64
+            )
             plane = keep.tile([P, width], U8, name=f"{name}_plane", align_bytes=64)
             nc.vector.quantize_mx(out=codes[:].bitcast(FP8X4), scales=plane[:], in_=grouped)
             return codes, plane
@@ -158,7 +163,6 @@ def tile_list_gaussian_atom_sites_kernel(
             a_bank, b_bank = banks[2 * h], banks[2 * h + 1]
             if h == 0:
                 gate[i] = ring.tile([P, S], F32, name="gate", bufs=2)
-                weighted[i] = ring.tile([P, S], F32, name="weighted", bufs=2)
             for a in range(PASSES):
                 gate_product(i, h, b_bank, a == 0, a == PASSES - 1, a)
             for a in range(PASSES):
@@ -176,14 +180,22 @@ def tile_list_gaussian_atom_sites_kernel(
             nc.scalar.activation(gate[i][:, cols], square[:], ACT.Exp, scale=-1.0)
 
         def weigh(i, h):
-            cols = slice(h * BANK, (h + 1) * BANK)
-            nc.vector.tensor_tensor(weighted[i][:, cols], banks[2 * h][:], weights[h][:], MULT)
+            if i == ROWS - 1:
+                half = keep.tile(
+                    [P, BANK], F32, name=f"weighted_last{h}", tag=f"last{h}", align_bytes=64
+                )
+                weighted[i, h, h + 1] = half[:]
+            else:
+                if h == 0:
+                    weighted[i, 0, 2] = ring.tile([P, S], F32, name="weighted", bufs=2)[:]
+                weighted[i, h, h + 1] = weighted[i, 0, 2][:, h * BANK : (h + 1) * BANK]
+            nc.vector.tensor_tensor(weighted[i, h, h + 1], banks[2 * h][:], weights[h][:], MULT)
 
         def scatter(i, first, last):
             cols = slice(first * BANK, last * BANK)
             nc.vector.tensor_tensor(
                 pages[i][:].indirect(places[:, first * COLS : last * COLS]),
-                weighted[i][:, cols],
+                weighted[i, first, last],
                 gate[i][:, cols],
                 MULT,
             )
@@ -242,10 +254,21 @@ def tile_list_gaussian_atom_sites_kernel(
                 weigh(i, 1)
                 wo_grouped = keep.tile([P, N, PACK], BF16, name="wo_grouped", align_bytes=64)
                 nc.scalar.copy(wo_grouped[:], wo_raw[:].rearrange("p i n -> p n i"))
+                scatter(i, 0, 1)
                 wo_codes, wo_plane = quantize(
-                    wo_grouped[:].rearrange("p n i -> p (n i)"), N, "wo"
+                    wo_grouped[:].rearrange("p n i -> p (n i)"), N, "wo", "last0"
                 )
-                scatter(i, 0, 2)
+                for bank in late_banks:
+                    nc.tensor.matmul_mx(
+                        out=bank[:],
+                        lhsT=wo_codes[:, :P].bitcast(FP8X4),
+                        lhsT_scale=wo_plane[:, :P],
+                        rhs=v_codes[0, 0].bitcast(FP8X4),
+                        rhs_scale=v_plane[0, 0][:],
+                        start=True,
+                        stop=True,
+                    )
+                scatter(i, 1, 2)
             if i < last:
                 for h in range(HALVES):
                     products(i + 1, h)
@@ -255,14 +278,17 @@ def tile_list_gaussian_atom_sites_kernel(
             for g in range(GROUPS):
                 round_z(i, g, "vector" if i == last and g % 2 == 0 else "scalar", into)
 
+        tail_banks = early_banks + late_banks
         z_grouped = {}
 
         def turn_back(g):
-            z_grouped[g] = ring.tile([P, BANK, PACK], BF16, name="z_grouped", align_bytes=64)
+            z_grouped[g] = keep.tile(
+                [P, BANK, PACK], BF16, name=f"z_grouped{g}", tag=f"spent{g}", align_bytes=64
+            )
             words = z_rows[g][:].bitcast(F32)
             grouped_words = z_grouped[g][:].rearrange("p t i -> p (t i)").bitcast(F32)
             for half in range(2):
-                bank = early_banks[2 * (g % 2) + half]
+                bank = tail_banks[2 * g + half]
                 for c2 in range(2):
                     for u in range(2):
                         col = (2 * c2 + u) * P
@@ -282,7 +308,7 @@ def tile_list_gaussian_atom_sites_kernel(
                 z_grouped[g][:].rearrange("p t i -> p (t i)"), BANK, f"z{g}"
             )
             for n in range(N // P):
-                bank = late_banks[2 * (g % 2) + n]
+                bank = tail_banks[2 * g + n]
                 nc.tensor.matmul_mx(
                     out=bank[:],
                     lhsT=wo_codes[:, n * P : (n + 1) * P].bitcast(FP8X4),

@@ -43,7 +43,8 @@ def tile_list_gaussian_atom_sites_kernel(
         atoms = lists.tile([P, S // 16], U16, name="atoms")
         places = lists.tile([P, S // 16], U16, name="places")
         table_words = [keep.tile([P, T], I32, name=f"table_words{a}") for a in range(PASSES)]
-        table_scales = keep.tile([P, PASSES, T // 4], I32, name="table_scales")
+        table_scales = keep.tile([P, T // 4], I32, name="table_scales")
+        v_planes = keep.tile([P, PASSES, S // 4], I32, name="v_planes", align_bytes=64)
         wa_codes = keep.tile([P, PASSES, 2 * H // 4], I32, name="wa_codes", align_bytes=64)
         wa_plane = keep.tile([P, PASSES, H // 4], I32, name="wa_plane", align_bytes=64)
         wg_first = [keep.tile([P, PACK, P], F32, name=f"wg_first{a}") for a in range(PASSES)]
@@ -66,7 +67,9 @@ def tile_list_gaussian_atom_sites_kernel(
                 table_words[a][:], tab_words[a].rearrange("p t i -> p (t i)").bitcast(I32)
             )
 
-        nc.vector.memset(table_scales[:], 0)
+        nc.vector.memset(table_scales[32:64, :], 0)
+        nc.vector.memset(table_scales[64:, :], 0)
+        nc.vector.memset(v_planes[:], 0)
         nc.gpsimd.memset(wa_plane[:], 0)
         nc.gpsimd.memset(warm[:], 0.0)
         nc.scalar.activation(warm[:], warm[:], ACT.Exp)
@@ -76,19 +79,15 @@ def tile_list_gaussian_atom_sites_kernel(
                 wa_scales[:, r:16:4, :].rearrange("a q c -> q a c").bitcast(I32),
             )
         make_identity(nc, identity[:])
-        for i in range(ROWS):
-            (nc.vector if i < 2 else nc.gpsimd).memset(pages[i][:], 0.0)
 
         nc.sync.dma_start(atoms[:], offs)
-        nc.sync.dma_start(places[:], offs2)
+        nc.sync.dma_start(
+            table_scales[:32, :], tab_scales.rearrange("a q t -> (a q) t").bitcast(I32)
+        )
         load_words(0)
-        for r in range(4):
-            nc.sync.dma_start(
-                table_scales[r:P:32, :, :],
-                tab_scales[:, r:16:4, :].rearrange("a q t -> q a t").bitcast(I32),
-            )
         for a in range(PASSES):
             nc.sync.dma_start(wg_first[a][:], wg_rows(a)[:, :, :P])
+        nc.sync.dma_start(places[:], offs2)
         load_words(1)
         nc.sync.dma_start(wa_codes[:], wa_words.rearrange("a p b -> p a b").bitcast(I32))
         nc.sync.dma_start(weights[0][:], wgs[:, :BANK])
@@ -102,12 +101,20 @@ def tile_list_gaussian_atom_sites_kernel(
 
         v_codes, v_plane = {}, {}
 
-        def gather_scales(a, h):
-            v_plane[a, h] = keep.tile([P, BANK], U8, name=f"v_plane{a}{h}", align_bytes=64)
-            nc.vector.tensor_copy(
-                v_plane[a, h][:],
-                table_scales[:, a, :].bitcast(U8).indirect(atoms[:, h * COLS : (h + 1) * COLS]),
-            )
+        picked_scales = keep.tile([P, S // 4], I32, name="picked_scales")
+        nc.vector.tensor_copy(
+            picked_scales[:].bitcast(U8), table_scales[:].bitcast(U8).indirect(atoms[:])
+        )
+        for a in range(PASSES):
+            for r in range(4):
+                nc.scalar.dma_start(
+                    v_planes[r:P:32, a, :], picked_scales[16 * a + r : 16 * (a + 1) : 4, :]
+                )
+            for h in range(HALVES):
+                v_plane[a, h] = v_planes[:, a, :].bitcast(U8)[:, h * BANK : (h + 1) * BANK]
+
+        for page in pages:
+            nc.vector.memset(page[:].bitcast(I32), 0)
 
         def gather_words(a, h, picked):
             v_codes[a, h] = picked[:, a, h * BANK : (h + 1) * BANK]
@@ -137,9 +144,6 @@ def tile_list_gaussian_atom_sites_kernel(
         picked = keep.tile([P, PASSES, S], U32, name="picked", align_bytes=64)
         for h in range(HALVES):
             gather_words(0, h, picked)
-        for h in range(HALVES):
-            for a in range(PASSES):
-                gather_scales(a, h)
         quantize_wg(0, [wg_first[a][:] for a in range(PASSES)])
         for h in range(HALVES):
             gather_words(1, h, picked)
@@ -153,7 +157,7 @@ def tile_list_gaussian_atom_sites_kernel(
                 lhsT=wg_codes[:, a * P : (a + 1) * P].bitcast(FP8X4),
                 lhsT_scale=wg_plane[:, a * P : (a + 1) * P],
                 rhs=v_codes[a, h].bitcast(FP8X4),
-                rhs_scale=v_plane[a, h][:],
+                rhs_scale=v_plane[a, h],
                 start=start,
                 stop=stop,
             )
@@ -171,7 +175,7 @@ def tile_list_gaussian_atom_sites_kernel(
                     lhsT=wa_codes[:, a, :].bitcast(U8)[:, 2 * i * P : 2 * (i + 1) * P].bitcast(FP4X4),
                     lhsT_scale=wa_plane[:, a, :].bitcast(U8)[:, i * P : (i + 1) * P],
                     rhs=v_codes[a, h].bitcast(FP8X4),
-                    rhs_scale=v_plane[a, h][:],
+                    rhs_scale=v_plane[a, h],
                     start=(a == 0),
                     stop=(a == PASSES - 1),
                 )
@@ -203,8 +207,8 @@ def tile_list_gaussian_atom_sites_kernel(
         early_banks = banks[4:]
         late_banks = [banks[1], banks[3], banks[0], banks[2]]
 
-        def turn(source, first, into):
-            for g in range(GROUPS):
+        def turn(source, first, into, groups=range(GROUPS)):
+            for g in groups:
                 for c in range(CHUNKS):
                     t0 = g * BANK + c * P
                     nc.tensor.matmul(
@@ -264,7 +268,7 @@ def tile_list_gaussian_atom_sites_kernel(
                         lhsT=wo_codes[:, :P].bitcast(FP8X4),
                         lhsT_scale=wo_plane[:, :P],
                         rhs=v_codes[0, 0].bitcast(FP8X4),
-                        rhs_scale=v_plane[0, 0][:],
+                        rhs_scale=v_plane[0, 0],
                         start=True,
                         stop=True,
                     )
@@ -274,14 +278,19 @@ def tile_list_gaussian_atom_sites_kernel(
                     products(i + 1, h)
             into = late_banks if i == last else early_banks
             turn(states[i][:], True, into)
-            turn(pages[i][:], False, into)
-            for g in range(GROUPS):
-                round_z(i, g, "vector" if i == last and g % 2 == 0 else "scalar", into)
+            if i < last:
+                turn(pages[i][:], False, into)
+                for g in range(GROUPS):
+                    round_z(i, g, "scalar", into)
 
         tail_banks = early_banks + late_banks
         z_grouped = {}
 
-        def turn_back(g):
+        def finish_rows(g, engine):
+            turn(pages[last][:], False, late_banks, [g])
+            round_z(last, g, engine, late_banks)
+
+        def turn_back(g, engines):
             z_grouped[g] = keep.tile(
                 [P, BANK, PACK], BF16, name=f"z_grouped{g}", tag=f"spent{g}", align_bytes=64
             )
@@ -296,34 +305,76 @@ def tile_list_gaussian_atom_sites_kernel(
                             bank[:, col : col + P], words[:, u, 2 * half + c2, :], identity[:]
                         )
                 copy_on(
-                    "scalar" if half == 0 else "vector",
+                    engines[half],
                     grouped_words[:, half * BANK : (half + 1) * BANK].rearrange(
                         "p (c t u) -> p c t u", c=2, u=2
                     ),
                     bank[:].rearrange("p (c u t) -> p c t u", c=2, u=2),
                 )
 
-        def project(g):
-            z_codes, z_plane = quantize(
-                z_grouped[g][:].rearrange("p t i -> p (t i)"), BANK, f"z{g}"
+        z_q = {}
+
+        def quantize_z(g, first, width):
+            z_q[g, first] = quantize(
+                z_grouped[g][:, first : first + width, :].rearrange("p t i -> p (t i)"),
+                width,
+                f"z{g}{first}",
             )
+
+        def project(g, first, n, target):
+            z_codes, z_plane = z_q[g, first]
+            nc.tensor.matmul_mx(
+                out=target,
+                lhsT=wo_codes[:, n * P : (n + 1) * P].bitcast(FP8X4),
+                lhsT_scale=wo_plane[:, n * P : (n + 1) * P],
+                rhs=z_codes[:].bitcast(FP8X4),
+                rhs_scale=z_plane[:],
+                start=True,
+                stop=True,
+            )
+
+        def project_group(g):
             for n in range(N // P):
-                bank = tail_banks[2 * g + n]
-                nc.tensor.matmul_mx(
-                    out=bank[:],
-                    lhsT=wo_codes[:, n * P : (n + 1) * P].bitcast(FP8X4),
-                    lhsT_scale=wo_plane[:, n * P : (n + 1) * P],
-                    rhs=z_codes[:].bitcast(FP8X4),
-                    rhs_scale=z_plane[:],
-                    start=True,
-                    stop=True,
-                )
+                project(g, 0, n, tail_banks[2 * g + n][:])
+
+        def store_group(g, engines):
+            for n in range(N // P):
                 result = keep.tile([P, BANK], F32, name=f"result{g}{n}")
-                copy_on("vector" if n == 1 and g >= 2 else "scalar", result[:], bank[:])
+                copy_on(engines[n], result[:], tail_banks[2 * g + n][:])
                 nc.sync.dma_start(out[n * P : (n + 1) * P, g * BANK : (g + 1) * BANK], result[:])
 
-        turn_back(0)
+        narrow = BANK // 2
+
+        def project_half(g, half):
+            for n in range(N // P):
+                project(g, half * narrow, n, tail_banks[2 * g + half][:, n * narrow : (n + 1) * narrow])
+
+        def store_half(g, half, engine):
+            result = keep.tile([P, BANK], F32, name=f"result{g}{half}")
+            copy_on(engine, result[:], tail_banks[2 * g + half][:])
+            t0 = g * BANK + half * narrow
+            nc.sync.dma_start(
+                out[:, t0 : t0 + narrow].rearrange("(n p) t -> p n t", p=P),
+                result[:].rearrange("p (n t) -> p n t", n=N // P),
+            )
+
         for g in range(GROUPS):
-            if g + 1 < GROUPS:
-                turn_back(g + 1)
-            project(g)
+            finish_rows(g, "scalar" if g == 1 else "vector")
+        turn_back(0, ("scalar", "vector"))
+        turn_back(1, ("scalar", "scalar"))
+        turn_back(2, ("scalar", "scalar"))
+        quantize_z(0, 0, BANK)
+        project_group(0)
+        turn_back(3, ("scalar", "scalar"))
+        quantize_z(1, 0, BANK)
+        project_group(1)
+        store_group(0, ("vector", "vector"))
+        quantize_z(2, 0, BANK)
+        project_group(2)
+        store_group(1, ("scalar", "scalar"))
+        for half in range(2):
+            quantize_z(3, half * narrow, narrow)
+            project_half(3, half)
+        store_group(2, ("vector", "vector"))
+        store_half(3, 0, "scalar")
+        store_half(3, 1, "scalar")

@@ -42,14 +42,16 @@ def tile_list_gaussian_atom_sites_kernel(
 
         atoms = lists.tile([P, S // 16], U16, name="atoms")
         places = lists.tile([P, S // 16], U16, name="places")
-        table_words = [keep.tile([P, T], I32, name=f"table_words{a}") for a in range(PASSES)]
+        table_words = [keep.tile([P, T], I32, name=f"table_words{a}", tag=f"table_words{a}") for a in range(PASSES)]
         table_scales = keep.tile([P, T // 4], I32, name="table_scales")
-        v_planes = keep.tile([P, PASSES, S // 4], I32, name="v_planes", align_bytes=64)
+        v_planes = [
+            keep.tile([P, S // 4], I32, name=f"v_planes{a}", align_bytes=64) for a in range(PASSES)
+        ]
         wa_codes = keep.tile([P, PASSES, 2 * H // 4], I32, name="wa_codes", align_bytes=64)
         wa_plane = keep.tile([P, PASSES, H // 4], I32, name="wa_plane", align_bytes=64)
-        wg_first = [keep.tile([P, PACK, P], F32, name=f"wg_first{a}") for a in range(PASSES)]
+        wg_first = [keep.tile([P, PACK, 2 * P], F32, name=f"wg_first{a}") for a in range(PASSES)]
         wg_rest = [
-            keep.tile([P, PACK, H - P], F32, name=f"wg_rest{a}", tag=f"spent{a}", align_bytes=64)
+            keep.tile([P, PACK, H - 2 * P], F32, name=f"wg_rest{a}", tag=f"spent{a}", align_bytes=64)
             for a in range(PASSES)
         ]
         weights = [keep.tile([P, BANK], F32, name=f"weights{h}") for h in range(HALVES)]
@@ -68,52 +70,57 @@ def tile_list_gaussian_atom_sites_kernel(
             )
 
         nc.vector.memset(table_scales[32:64, :], 0)
-        nc.vector.memset(table_scales[64:, :], 0)
-        nc.vector.memset(v_planes[:], 0)
+        for a in range(PASSES):
+            nc.vector.memset(v_planes[a][:], 0)
         nc.gpsimd.memset(wa_plane[:], 0)
         nc.gpsimd.memset(warm[:], 0.0)
+        nc.gpsimd.memset(table_scales[64:, :], 0)
         nc.scalar.activation(warm[:], warm[:], ACT.Exp)
         for r in range(4):
-            nc.gpsimd.dma_start(
+            nc.scalar.dma_start(
                 wa_plane[r:P:32, :, :],
                 wa_scales[:, r:16:4, :].rearrange("a q c -> q a c").bitcast(I32),
             )
-        make_identity(nc, identity[:])
 
         nc.sync.dma_start(atoms[:], offs)
         nc.sync.dma_start(
             table_scales[:32, :], tab_scales.rearrange("a q t -> (a q) t").bitcast(I32)
         )
-        load_words(0)
-        for a in range(PASSES):
-            nc.sync.dma_start(wg_first[a][:], wg_rows(a)[:, :, :P])
         nc.sync.dma_start(places[:], offs2)
-        load_words(1)
-        nc.sync.dma_start(wa_codes[:], wa_words.rearrange("a p b -> p a b").bitcast(I32))
-        nc.sync.dma_start(weights[0][:], wgs[:, :BANK])
         for a in range(PASSES):
-            nc.sync.dma_start(wg_rest[a][:], wg_rows(a)[:, :, P:])
-        nc.sync.dma_start(weights[1][:], wgs[:, BANK:])
-        nc.sync.dma_start(states[0][:], sites[:P, :])
-        nc.sync.dma_start(wo_raw[:], wo.rearrange("(p i) n -> p i n", i=PACK))
-        for i in range(1, ROWS):
-            nc.sync.dma_start(states[i][:], sites[i * P : (i + 1) * P, :])
-
+            nc.sync.dma_start(wg_first[a][:], wg_rows(a)[:, :, : 2 * P])
+        load_words(0)
         v_codes, v_plane = {}, {}
 
         picked_scales = keep.tile([P, S // 4], I32, name="picked_scales")
         nc.vector.tensor_copy(
             picked_scales[:].bitcast(U8), table_scales[:].bitcast(U8).indirect(atoms[:])
         )
-        for a in range(PASSES):
-            for r in range(4):
-                nc.scalar.dma_start(
-                    v_planes[r:P:32, a, :], picked_scales[16 * a + r : 16 * (a + 1) : 4, :]
-                )
-            for h in range(HALVES):
-                v_plane[a, h] = v_planes[:, a, :].bitcast(U8)[:, h * BANK : (h + 1) * BANK]
+        moves = [(a, r) for a in range(PASSES) for r in range(4)]
 
-        for page in pages:
+        def move_scales(a, r):
+            nc.sync.dma_start(v_planes[a][r:P:32, :], picked_scales[16 * a + r : 16 * (a + 1) : 4, :])
+
+        for a, r in moves[:6]:
+            move_scales(a, r)
+        load_words(1)
+        for a, r in moves[6:]:
+            move_scales(a, r)
+        for a in range(PASSES):
+            for h in range(HALVES):
+                v_plane[a, h] = v_planes[a][:].bitcast(U8)[:, h * BANK : (h + 1) * BANK]
+        nc.sync.dma_start(wa_codes[:], wa_words.rearrange("a p b -> p a b").bitcast(I32))
+        nc.sync.dma_start(weights[0][:], wgs[:, :BANK])
+        for a in range(PASSES):
+            nc.sync.dma_start(wg_rest[a][:], wg_rows(a)[:, :, 2 * P :])
+        nc.sync.dma_start(weights[1][:], wgs[:, BANK:])
+        nc.sync.dma_start(states[0][:], sites[:P, :])
+        nc.sync.dma_start(wo_raw[:], wo.rearrange("(p i) n -> p i n", i=PACK))
+        for i in range(1, ROWS):
+            nc.sync.dma_start(states[i][:], sites[i * P : (i + 1) * P, :])
+
+        make_identity(nc, identity[:])
+        for i, page in enumerate(pages):
             nc.vector.memset(page[:].bitcast(I32), 0)
 
         def gather_words(a, h, picked):
@@ -144,11 +151,11 @@ def tile_list_gaussian_atom_sites_kernel(
         picked = keep.tile([P, PASSES, S], U32, name="picked", align_bytes=64)
         for h in range(HALVES):
             gather_words(0, h, picked)
-        quantize_wg(0, [wg_first[a][:] for a in range(PASSES)])
+        for i in range(2):
+            quantize_wg(i, [wg_first[a][:, :, i * P : (i + 1) * P] for a in range(PASSES)])
         for h in range(HALVES):
             gather_words(1, h, picked)
 
-        gate, weighted = {}, {}
 
         def gate_product(i, h, bank, start, stop, a):
             wg_codes, wg_plane = wg_q[i]
@@ -162,11 +169,13 @@ def tile_list_gaussian_atom_sites_kernel(
                 stop=stop,
             )
 
+        product_banks = banks[:4]
+        sum_banks = banks[4:]
+        messages = {}
+
         def products(i, h):
-            cols = slice(h * BANK, (h + 1) * BANK)
-            a_bank, b_bank = banks[2 * h], banks[2 * h + 1]
-            if h == 0:
-                gate[i] = ring.tile([P, S], F32, name="gate", bufs=2)
+            own = sum_banks if i == 1 else product_banks
+            a_bank, b_bank = own[2 * h], own[2 * h + 1]
             for a in range(PASSES):
                 gate_product(i, h, b_bank, a == 0, a == PASSES - 1, a)
             for a in range(PASSES):
@@ -180,31 +189,35 @@ def tile_list_gaussian_atom_sites_kernel(
                     stop=(a == PASSES - 1),
                 )
             square = ring.tile([P, BANK], F32, name="square", bufs=2)
+            gate = ring.tile([P, BANK], F32, name="gate", bufs=2)
+            factor = ring.tile([P, BANK], F32, name="factor", bufs=2)
             nc.scalar.activation(square[:], b_bank[:], ACT.Square)
-            nc.scalar.activation(gate[i][:, cols], square[:], ACT.Exp, scale=-1.0)
-
-        def weigh(i, h):
+            nc.scalar.activation(gate[:], square[:], ACT.Exp, scale=-1.0)
             if i == ROWS - 1:
                 half = keep.tile(
-                    [P, BANK], F32, name=f"weighted_last{h}", tag=f"last{h}", align_bytes=64
+                    [P, BANK], F32, name=f"message_last{h}", tag=f"last{h}", align_bytes=64
                 )
-                weighted[i, h, h + 1] = half[:]
+                messages[i, h, h + 1] = half[:]
             else:
                 if h == 0:
-                    weighted[i, 0, 2] = ring.tile([P, S], F32, name="weighted", bufs=2)[:]
-                weighted[i, h, h + 1] = weighted[i, 0, 2][:, h * BANK : (h + 1) * BANK]
-            nc.vector.tensor_tensor(weighted[i, h, h + 1], banks[2 * h][:], weights[h][:], MULT)
+                    messages[i, 0, 2] = keep.tile([P, S], F32, name=f"message{i}")[:]
+                messages[i, h, h + 1] = messages[i, 0, 2][:, h * BANK : (h + 1) * BANK]
+            if (i, h) == (0, 0):
+                nc.vector.tensor_tensor(factor[:], a_bank[:], weights[h][:], MULT)
+                nc.vector.tensor_tensor(messages[i, h, h + 1], factor[:], gate[:], MULT)
+            else:
+                raw = ring.tile([P, BANK], F32, name="raw", bufs=2)
+                nc.scalar.copy(raw[:], a_bank[:])
+                nc.gpsimd.tensor_tensor(factor[:], gate[:], weights[h][:], MULT)
+                nc.gpsimd.tensor_tensor(messages[i, h, h + 1], factor[:], raw[:], MULT)
 
         def scatter(i, first, last):
-            cols = slice(first * BANK, last * BANK)
-            nc.vector.tensor_tensor(
+            nc.vector.tensor_copy(
                 pages[i][:].indirect(places[:, first * COLS : last * COLS]),
-                weighted[i, first, last],
-                gate[i][:, cols],
-                MULT,
+                messages[i, first, last],
             )
 
-        early_banks = banks[4:]
+        early_banks = sum_banks
         late_banks = [banks[1], banks[3], banks[0], banks[2]]
 
         def turn(source, first, into, groups=range(GROUPS)):
@@ -220,7 +233,15 @@ def tile_list_gaussian_atom_sites_kernel(
                         stop=(not first and c == CHUNKS - 1),
                     )
 
-        z_rows = [keep.tile([P, 2, CHUNKS, 2 * P], BF16, name=f"z_rows{g}") for g in range(GROUPS)]
+        z_rows = [
+            keep.tile(
+                [P, 2, CHUNKS, 2 * P],
+                BF16,
+                name=f"z_rows{g}",
+                tag=f"table_words{g}" if g < PASSES else f"z_rows{g}",
+            )
+            for g in range(GROUPS)
+        ]
 
         def copy_on(engine, dst, src):
             if engine == "vector":
@@ -236,52 +257,49 @@ def tile_list_gaussian_atom_sites_kernel(
             )
 
         def next_wg(i):
-            quantize_wg(i, [wg_rest[a][:, :, (i - 1) * P : i * P] for a in range(PASSES)])
+            quantize_wg(i, [wg_rest[a][:, :, (i - 2) * P : (i - 1) * P] for a in range(PASSES)])
 
         last = ROWS - 1
-        for h in range(HALVES):
-            products(0, h)
-        for i in range(ROWS):
-            if i == 0:
-                weigh(i, 0)
-                scatter(i, 0, 1)
-                weigh(i, 1)
+
+        def sum_rows(i):
+            for g in range(GROUPS):
+                turn(states[i][:], True, early_banks, [g])
+                turn(pages[i][:], False, early_banks, [g])
+                round_z(i, g, "scalar", early_banks)
+
+        products(0, 0)
+        scatter(0, 0, 1)
+        products(0, 1)
+        scatter(0, 1, 2)
+        for i in range(1, ROWS):
+            if i < last:
                 next_wg(i + 1)
-                scatter(i, 1, 2)
-            elif i < last:
-                weigh(i, 0)
-                weigh(i, 1)
-                next_wg(i + 1)
-                scatter(i, 0, 2)
             else:
-                weigh(i, 0)
-                weigh(i, 1)
                 wo_grouped = keep.tile([P, N, PACK], BF16, name="wo_grouped", align_bytes=64)
                 nc.scalar.copy(wo_grouped[:], wo_raw[:].rearrange("p i n -> p n i"))
-                scatter(i, 0, 1)
-                wo_codes, wo_plane = quantize(
-                    wo_grouped[:].rearrange("p n i -> p (n i)"), N, "wo", "last0"
-                )
-                for bank in late_banks:
-                    nc.tensor.matmul_mx(
-                        out=bank[:],
-                        lhsT=wo_codes[:, :P].bitcast(FP8X4),
-                        lhsT_scale=wo_plane[:, :P],
-                        rhs=v_codes[0, 0].bitcast(FP8X4),
-                        rhs_scale=v_plane[0, 0],
-                        start=True,
-                        stop=True,
-                    )
-                scatter(i, 1, 2)
-            if i < last:
-                for h in range(HALVES):
-                    products(i + 1, h)
-            into = late_banks if i == last else early_banks
-            turn(states[i][:], True, into)
-            if i < last:
-                turn(pages[i][:], False, into)
-                for g in range(GROUPS):
-                    round_z(i, g, "scalar", into)
+            for h in range(HALVES):
+                products(i, h)
+                if i < last:
+                    scatter(i, h, h + 1)
+            if i >= 2:
+                sum_rows(i - 2)
+        sum_rows(last - 1)
+        scatter(last, 0, 1)
+        wo_codes, wo_plane = quantize(
+            wo_grouped[:].rearrange("p n i -> p (n i)"), N, "wo", "last0"
+        )
+        for bank in late_banks:
+            nc.tensor.matmul_mx(
+                out=bank[:],
+                lhsT=wo_codes[:, :P].bitcast(FP8X4),
+                lhsT_scale=wo_plane[:, :P],
+                rhs=v_codes[0, 0].bitcast(FP8X4),
+                rhs_scale=v_plane[0, 0],
+                start=True,
+                stop=True,
+            )
+        scatter(last, 1, 2)
+        turn(states[last][:], True, late_banks)
 
         tail_banks = early_banks + late_banks
         z_grouped = {}

@@ -26,6 +26,7 @@ ROWS = H // P
 GROUPS = T2 // BANK
 CHUNKS = BANK // P
 COLS = BANK // 16
+PAGES = 3
 
 
 def tile_list_gaussian_atom_sites_kernel(
@@ -56,7 +57,8 @@ def tile_list_gaussian_atom_sites_kernel(
         ]
         weights = [keep.tile([P, BANK], F32, name=f"weights{h}") for h in range(HALVES)]
         states = [keep.tile([P, T2], F32, name=f"states{i}") for i in range(ROWS)]
-        pages = [keep.tile([P, T2], F32, name=f"pages{i}") for i in range(ROWS)]
+        page_tiles = [keep.tile([P, T2], F32, name=f"pages{i}") for i in range(PAGES)]
+        pages = [page_tiles[i % PAGES] for i in range(ROWS)]
         wo_raw = keep.tile([P, PACK, N], F32, name="wo_raw")
         identity = keep.tile([P, P], F32, name="identity")
         warm = keep.tile([P, 8], F32, name="warm")
@@ -120,7 +122,7 @@ def tile_list_gaussian_atom_sites_kernel(
             nc.sync.dma_start(states[i][:], sites[i * P : (i + 1) * P, :])
 
         make_identity(nc, identity[:])
-        for i, page in enumerate(pages):
+        for page in page_tiles:
             nc.vector.memset(page[:].bitcast(I32), 0)
 
         def gather_words(a, h, picked):
@@ -144,9 +146,13 @@ def tile_list_gaussian_atom_sites_kernel(
             grouped = keep.tile([P, PASSES, P, PACK], BF16, name=f"wg_grouped{i}", align_bytes=64)
             for a in range(PASSES):
                 nc.scalar.copy(grouped[:, a, :, :], raw[a].rearrange("p i r -> p r i"))
-            wg_q[i] = quantize(
+            codes, plane = quantize(
                 grouped[:].rearrange("p a r i -> p (a r i)"), PASSES * P, f"wg{i}"
             )
+            wg_q[i] = (codes[:], plane[:])
+
+        def next_wg(i):
+            quantize_wg(i, [wg_rest[a][:, :, (i - 2) * P : (i - 1) * P] for a in range(PASSES)])
 
         picked = keep.tile([P, PASSES, S], U32, name="picked", align_bytes=64)
         for h in range(HALVES):
@@ -156,82 +162,80 @@ def tile_list_gaussian_atom_sites_kernel(
         for h in range(HALVES):
             gather_words(1, h, picked)
 
-
-        def gate_product(i, h, bank, start, stop, a):
-            wg_codes, wg_plane = wg_q[i]
-            nc.tensor.matmul_mx(
-                out=bank[:],
-                lhsT=wg_codes[:, a * P : (a + 1) * P].bitcast(FP8X4),
-                lhsT_scale=wg_plane[:, a * P : (a + 1) * P],
-                rhs=v_codes[a, h].bitcast(FP8X4),
-                rhs_scale=v_plane[a, h],
-                start=start,
-                stop=stop,
-            )
-
         product_banks = banks[:4]
         sum_banks = banks[4:]
         messages = {}
 
-        def products(i, h):
+        def own_banks(i, h):
             own = sum_banks if i == 1 else product_banks
-            a_bank, b_bank = own[2 * h], own[2 * h + 1]
-            for a in range(PASSES):
-                gate_product(i, h, b_bank, a == 0, a == PASSES - 1, a)
-            for a in range(PASSES):
-                nc.tensor.matmul_mx(
-                    out=a_bank[:],
-                    lhsT=wa_codes[:, a, :].bitcast(U8)[:, 2 * i * P : 2 * (i + 1) * P].bitcast(FP4X4),
-                    lhsT_scale=wa_plane[:, a, :].bitcast(U8)[:, i * P : (i + 1) * P],
-                    rhs=v_codes[a, h].bitcast(FP8X4),
-                    rhs_scale=v_plane[a, h],
-                    start=(a == 0),
-                    stop=(a == PASSES - 1),
-                )
-            square = ring.tile([P, BANK], F32, name="square", bufs=2)
-            gate = ring.tile([P, BANK], F32, name="gate", bufs=2)
-            factor = ring.tile([P, BANK], F32, name="factor", bufs=2)
-            nc.scalar.activation(square[:], b_bank[:], ACT.Square)
-            nc.scalar.activation(gate[:], square[:], ACT.Exp, scale=-1.0)
-            if i == ROWS - 1:
-                half = keep.tile(
-                    [P, BANK], F32, name=f"message_last{h}", tag=f"last{h}", align_bytes=64
-                )
-                messages[i, h, h + 1] = half[:]
-            else:
-                if h == 0:
-                    messages[i, 0, 2] = keep.tile([P, S], F32, name=f"message{i}")[:]
-                messages[i, h, h + 1] = messages[i, 0, 2][:, h * BANK : (h + 1) * BANK]
-            if (i, h) == (0, 0):
-                nc.vector.tensor_tensor(factor[:], a_bank[:], weights[h][:], MULT)
-                nc.vector.tensor_tensor(messages[i, h, h + 1], factor[:], gate[:], MULT)
-            else:
-                raw = ring.tile([P, BANK], F32, name="raw", bufs=2)
-                nc.scalar.copy(raw[:], a_bank[:])
-                nc.gpsimd.tensor_tensor(factor[:], gate[:], weights[h][:], MULT)
-                nc.gpsimd.tensor_tensor(messages[i, h, h + 1], factor[:], raw[:], MULT)
+            return own[2 * h], own[2 * h + 1]
 
-        def scatter(i, first, last):
-            nc.vector.tensor_copy(
-                pages[i][:].indirect(places[:, first * COLS : last * COLS]),
-                messages[i, first, last],
+        def gate_pass(i, h, a):
+            wg_codes, wg_plane = wg_q[i]
+            nc.tensor.matmul_mx(
+                out=own_banks(i, h)[1][:],
+                lhsT=wg_codes[:, a * P : (a + 1) * P].bitcast(FP8X4),
+                lhsT_scale=wg_plane[:, a * P : (a + 1) * P],
+                rhs=v_codes[a, h].bitcast(FP8X4),
+                rhs_scale=v_plane[a, h],
+                start=(a == 0),
+                stop=(a == PASSES - 1),
             )
 
-        early_banks = sum_banks
-        late_banks = [banks[1], banks[3], banks[0], banks[2]]
+        def message_pass(i, h, a):
+            nc.tensor.matmul_mx(
+                out=own_banks(i, h)[0][:],
+                lhsT=wa_codes[:, a, :].bitcast(U8)[:, 2 * i * P : 2 * (i + 1) * P].bitcast(FP4X4),
+                lhsT_scale=wa_plane[:, a, :].bitcast(U8)[:, i * P : (i + 1) * P],
+                rhs=v_codes[a, h].bitcast(FP8X4),
+                rhs_scale=v_plane[a, h],
+                start=(a == 0),
+                stop=(a == PASSES - 1),
+            )
 
-        def turn(source, first, into, groups=range(GROUPS)):
-            for g in groups:
-                for c in range(CHUNKS):
-                    t0 = g * BANK + c * P
-                    nc.tensor.matmul(
-                        into[g][:, c * P : (c + 1) * P],
-                        lhsT=source[:, t0 : t0 + P],
-                        rhs=identity[:],
-                        is_transpose=True,
-                        start=(first and c == 0),
-                        stop=(not first and c == CHUNKS - 1),
-                    )
+        gates = {}
+
+        def gate_of(i, h, passes=range(PASSES)):
+            for a in passes:
+                gate_pass(i, h, a)
+            square = ring.tile([P, BANK], F32, name="square", bufs=2)
+            gates[i, h] = ring.tile([P, BANK], F32, name="gate", bufs=3)
+            nc.scalar.activation(square[:], own_banks(i, h)[1][:], ACT.Square)
+            nc.scalar.activation(gates[i, h][:], square[:], ACT.Exp, scale=-1.0)
+
+        def message_of(i, h, passes=range(PASSES)):
+            for a in passes:
+                message_pass(i, h, a)
+            a_bank = own_banks(i, h)[0]
+            factor = ring.tile([P, BANK], F32, name="factor", bufs=2)
+            messages[i, h] = keep.tile(
+                [P, BANK], F32, name=f"message{i}{h}", tag=f"message{i}{h}", align_bytes=64
+            )
+            if (i, h) == (0, 0):
+                nc.vector.tensor_tensor(factor[:], a_bank[:], weights[h][:], MULT)
+                nc.vector.tensor_tensor(messages[i, h][:], factor[:], gates[i, h][:], MULT)
+            else:
+                raw = ring.tile([P, BANK], F32, name="raw", bufs=3)
+                nc.scalar.copy(raw[:], a_bank[:])
+                nc.gpsimd.tensor_tensor(factor[:], gates[i, h][:], weights[h][:], MULT)
+                nc.gpsimd.tensor_tensor(messages[i, h][:], factor[:], raw[:], MULT)
+
+        def scatter(i, h):
+            nc.vector.tensor_copy(
+                pages[i][:].indirect(places[:, h * COLS : (h + 1) * COLS]), messages[i, h][:]
+            )
+
+        def turn(source, first, bank, g):
+            for c in range(CHUNKS):
+                t0 = g * BANK + c * P
+                nc.tensor.matmul(
+                    bank[:, c * P : (c + 1) * P],
+                    lhsT=source[:, t0 : t0 + P],
+                    rhs=identity[:],
+                    is_transpose=True,
+                    start=(first and c == 0),
+                    stop=(not first and c == CHUNKS - 1),
+                )
 
         z_rows = [
             keep.tile(
@@ -256,39 +260,61 @@ def tile_list_gaussian_atom_sites_kernel(
                 into[g][:].rearrange("p (c m u e) -> p u c m e", c=CHUNKS, u=2, e=2),
             )
 
-        def next_wg(i):
-            quantize_wg(i, [wg_rest[a][:, :, (i - 2) * P : (i - 1) * P] for a in range(PASSES)])
-
         last = ROWS - 1
+        late_banks = [banks[1], banks[0], banks[3], banks[2]]
 
-        def sum_rows(i):
-            for g in range(GROUPS):
-                turn(states[i][:], True, early_banks, [g])
-                turn(pages[i][:], False, early_banks, [g])
-                round_z(i, g, "scalar", early_banks)
+        def sums_of(i):
+            return late_banks if i == last else sum_banks
 
-        products(0, 0)
-        scatter(0, 0, 1)
-        products(0, 1)
-        scatter(0, 1, 2)
-        for i in range(1, ROWS):
-            if i < last:
-                next_wg(i + 1)
-            else:
-                wo_grouped = keep.tile([P, N, PACK], BF16, name="wo_grouped", align_bytes=64)
-                nc.scalar.copy(wo_grouped[:], wo_raw[:].rearrange("p i n -> p n i"))
+        def turn_sites(i, g):
+            turn(states[i][:], True, sums_of(i)[g], g)
+
+        def turn_page(i, g, engine="scalar"):
+            turn(pages[i][:], False, sums_of(i)[g], g)
+            round_z(i, g, engine, sums_of(i))
+
+        for i in range(2):
             for h in range(HALVES):
-                products(i, h)
-                if i < last:
-                    scatter(i, h, h + 1)
-            if i >= 2:
-                sum_rows(i - 2)
-        sum_rows(last - 1)
-        scatter(last, 0, 1)
+                gate_pass(i, h, 0)
+        message_pass(0, 0, 0)
+        gate_of(0, 0, [1])
+        message_of(0, 0, [1])
+        scatter(0, 0)
+        gate_of(0, 1, [1])
+        message_of(0, 1)
+        for h in range(HALVES):
+            gate_of(1, h, [1])
+            message_of(1, h)
+            next_wg(2 + h)
+        scatter(0, 1)
+        for g in range(GROUPS):
+            turn_sites(0, g)
+        for i in range(1, last):
+            scatter(i, 0)
+            gate_of(i + 1, 0)
+            turn_page(i - 1, 0)
+            turn_page(i - 1, 1)
+            message_of(i + 1, 0)
+            turn_sites(i, 0)
+            turn_page(i - 1, 2)
+            scatter(i, 1)
+            gate_of(i + 1, 1)
+            turn_sites(i, 1)
+            turn_page(i - 1, 3)
+            message_of(i + 1, 1)
+            turn_sites(i, 2)
+            turn_sites(i, 3)
+        scatter(last, 0)
+        for g in range(GROUPS):
+            turn_sites(last, g)
+        wo_grouped = keep.tile([P, N, PACK], BF16, name="wo_grouped", align_bytes=64)
+        nc.scalar.copy(wo_grouped[:], wo_raw[:].rearrange("p i n -> p n i"))
+        for g in range(GROUPS):
+            turn_page(last - 1, g)
         wo_codes, wo_plane = quantize(
-            wo_grouped[:].rearrange("p n i -> p (n i)"), N, "wo", "last0"
+            wo_grouped[:].rearrange("p n i -> p (n i)"), N, "wo", f"message{last}0"
         )
-        for bank in late_banks:
+        for bank in sum_banks:
             nc.tensor.matmul_mx(
                 out=bank[:],
                 lhsT=wo_codes[:, :P].bitcast(FP8X4),
@@ -298,15 +324,10 @@ def tile_list_gaussian_atom_sites_kernel(
                 start=True,
                 stop=True,
             )
-        scatter(last, 1, 2)
-        turn(states[last][:], True, late_banks)
+        scatter(last, 1)
 
-        tail_banks = early_banks + late_banks
+        tail_banks = sum_banks + late_banks
         z_grouped = {}
-
-        def finish_rows(g, engine):
-            turn(pages[last][:], False, late_banks, [g])
-            round_z(last, g, engine, late_banks)
 
         def turn_back(g, engines):
             z_grouped[g] = keep.tile(
@@ -361,38 +382,21 @@ def tile_list_gaussian_atom_sites_kernel(
                 copy_on(engines[n], result[:], tail_banks[2 * g + n][:])
                 nc.sync.dma_start(out[n * P : (n + 1) * P, g * BANK : (g + 1) * BANK], result[:])
 
-        narrow = BANK // 2
-
-        def project_half(g, half):
-            for n in range(N // P):
-                project(g, half * narrow, n, tail_banks[2 * g + half][:, n * narrow : (n + 1) * narrow])
-
-        def store_half(g, half, engine):
-            result = keep.tile([P, BANK], F32, name=f"result{g}{half}")
-            copy_on(engine, result[:], tail_banks[2 * g + half][:])
-            t0 = g * BANK + half * narrow
-            nc.sync.dma_start(
-                out[:, t0 : t0 + narrow].rearrange("(n p) t -> p n t", p=P),
-                result[:].rearrange("p (n t) -> p n t", n=N // P),
-            )
-
         for g in range(GROUPS):
-            finish_rows(g, "scalar" if g == 1 else "vector")
-        turn_back(0, ("scalar", "vector"))
-        turn_back(1, ("scalar", "scalar"))
-        turn_back(2, ("scalar", "scalar"))
+            turn_page(last, g, "scalar" if g % 2 else "vector")
+        turn_back(0, ("vector", "scalar"))
+        turn_back(1, ("vector", "scalar"))
         quantize_z(0, 0, BANK)
+        turn_back(2, ("scalar", "vector"))
         project_group(0)
-        turn_back(3, ("scalar", "scalar"))
         quantize_z(1, 0, BANK)
+        turn_back(3, ("vector", "scalar"))
         project_group(1)
-        store_group(0, ("vector", "vector"))
         quantize_z(2, 0, BANK)
+        store_group(0, ("scalar", "scalar"))
         project_group(2)
-        store_group(1, ("scalar", "scalar"))
-        for half in range(2):
-            quantize_z(3, half * narrow, narrow)
-            project_half(3, half)
-        store_group(2, ("vector", "vector"))
-        store_half(3, 0, "scalar")
-        store_half(3, 1, "scalar")
+        store_group(1, ("vector", "scalar"))
+        quantize_z(3, 0, BANK)
+        project_group(3)
+        store_group(2, ("scalar", "vector"))
+        store_group(3, ("scalar", "vector"))

@@ -78,20 +78,20 @@ def tile_list_gaussian_atom_sites_kernel(
         nc.gpsimd.memset(warm[:], 0.0)
         nc.gpsimd.memset(table_scales[64:, :], 0)
         nc.scalar.activation(warm[:], warm[:], ACT.Exp)
-        for r in range(4):
-            nc.scalar.dma_start(
-                wa_plane[r:P:32, :, :],
-                wa_scales[:, r:16:4, :].rearrange("a q c -> q a c").bitcast(I32),
-            )
 
-        nc.sync.dma_start(atoms[:], offs)
         nc.sync.dma_start(
             table_scales[:32, :], tab_scales.rearrange("a q t -> (a q) t").bitcast(I32)
         )
-        nc.sync.dma_start(places[:], offs2)
+        nc.sync.dma_start(atoms[:], offs)
+        load_words(0)
+        for r in range(4):
+            nc.sync.dma_start(
+                wa_plane[r:P:32, :, :],
+                wa_scales[:, r:16:4, :].rearrange("a q c -> q a c").bitcast(I32),
+            )
+        nc.sync.dma_start(wa_codes[:], wa_words.rearrange("a p b -> p a b").bitcast(I32))
         for a in range(PASSES):
             nc.sync.dma_start(wg_first[a][:], wg_rows(a)[:, :, : 2 * P])
-        load_words(0)
         v_codes, v_plane = {}, {}
 
         picked_scales = keep.tile([P, S // 4], I32, name="picked_scales")
@@ -103,15 +103,15 @@ def tile_list_gaussian_atom_sites_kernel(
         def move_scales(a, r):
             nc.sync.dma_start(v_planes[a][r:P:32, :], picked_scales[16 * a + r : 16 * (a + 1) : 4, :])
 
-        for a, r in moves[:6]:
+        for a, r in moves[:5]:
             move_scales(a, r)
         load_words(1)
-        for a, r in moves[6:]:
+        for a, r in moves[5:]:
             move_scales(a, r)
         for a in range(PASSES):
             for h in range(HALVES):
                 v_plane[a, h] = v_planes[a][:].bitcast(U8)[:, h * BANK : (h + 1) * BANK]
-        nc.sync.dma_start(wa_codes[:], wa_words.rearrange("a p b -> p a b").bitcast(I32))
+        nc.sync.dma_start(places[:], offs2)
         nc.sync.dma_start(weights[0][:], wgs[:, :BANK])
         for a in range(PASSES):
             nc.sync.dma_start(wg_rest[a][:], wg_rows(a)[:, :, 2 * P :])
@@ -123,7 +123,8 @@ def tile_list_gaussian_atom_sites_kernel(
 
         make_identity(nc, identity[:])
         for page in page_tiles:
-            nc.vector.memset(page[:].bitcast(I32), 0)
+            for g in range(GROUPS):
+                nc.vector.memset(page[:, g * BANK : (g + 1) * BANK].bitcast(I32), 0)
 
         def gather_words(a, h, picked):
             v_codes[a, h] = picked[:, a, h * BANK : (h + 1) * BANK]
@@ -199,7 +200,7 @@ def tile_list_gaussian_atom_sites_kernel(
             for a in passes:
                 gate_pass(i, h, a)
             square = ring.tile([P, BANK], F32, name="square", bufs=2)
-            gates[i, h] = ring.tile([P, BANK], F32, name="gate", bufs=3)
+            gates[i, h] = ring.tile([P, BANK], F32, name="gate", bufs=8)
             nc.scalar.activation(square[:], own_banks(i, h)[1][:], ACT.Square)
             nc.scalar.activation(gates[i, h][:], square[:], ACT.Exp, scale=-1.0)
 
@@ -215,7 +216,7 @@ def tile_list_gaussian_atom_sites_kernel(
                 nc.vector.tensor_tensor(factor[:], a_bank[:], weights[h][:], MULT)
                 nc.vector.tensor_tensor(messages[i, h][:], factor[:], gates[i, h][:], MULT)
             else:
-                raw = ring.tile([P, BANK], F32, name="raw", bufs=3)
+                raw = ring.tile([P, BANK], F32, name="raw", bufs=7)
                 nc.scalar.copy(raw[:], a_bank[:])
                 nc.gpsimd.tensor_tensor(factor[:], gates[i, h][:], weights[h][:], MULT)
                 nc.gpsimd.tensor_tensor(messages[i, h][:], factor[:], raw[:], MULT)
@@ -261,7 +262,7 @@ def tile_list_gaussian_atom_sites_kernel(
             )
 
         last = ROWS - 1
-        late_banks = [banks[1], banks[0], banks[3], banks[2]]
+        late_banks = [banks[1], banks[3], banks[0], banks[2]]
 
         def sums_of(i):
             return late_banks if i == last else sum_banks
@@ -273,40 +274,38 @@ def tile_list_gaussian_atom_sites_kernel(
             turn(pages[i][:], False, sums_of(i)[g], g)
             round_z(i, g, engine, sums_of(i))
 
+        def products(i, h, passes=range(PASSES)):
+            gate_of(i, h, passes)
+            message_of(i, h, passes)
+
         for i in range(2):
             for h in range(HALVES):
                 gate_pass(i, h, 0)
-        message_pass(0, 0, 0)
+                message_pass(i, h, 0)
         gate_of(0, 0, [1])
         message_of(0, 0, [1])
         scatter(0, 0)
-        gate_of(0, 1, [1])
-        message_of(0, 1)
-        for h in range(HALVES):
-            gate_of(1, h, [1])
-            message_of(1, h)
-            next_wg(2 + h)
+        products(0, 1, [1])
+        next_wg(2)
         scatter(0, 1)
-        for g in range(GROUPS):
-            turn_sites(0, g)
-        for i in range(1, last):
+        products(1, 0, [1])
+        next_wg(3)
+        scatter(1, 0)
+        products(1, 1, [1])
+        scatter(1, 1)
+        for i in range(2, ROWS):
+            for h in range(HALVES):
+                products(i, h)
+            if i == 2:
+                for g in range(GROUPS):
+                    turn_sites(0, g)
+            for g in range(GROUPS):
+                turn_page(i - 2, g)
+            for g in range(GROUPS):
+                turn_sites(i - 1, g)
             scatter(i, 0)
-            gate_of(i + 1, 0)
-            turn_page(i - 1, 0)
-            turn_page(i - 1, 1)
-            message_of(i + 1, 0)
-            turn_sites(i, 0)
-            turn_page(i - 1, 2)
-            scatter(i, 1)
-            gate_of(i + 1, 1)
-            turn_sites(i, 1)
-            turn_page(i - 1, 3)
-            message_of(i + 1, 1)
-            turn_sites(i, 2)
-            turn_sites(i, 3)
-        scatter(last, 0)
-        for g in range(GROUPS):
-            turn_sites(last, g)
+            if i < last:
+                scatter(i, 1)
         wo_grouped = keep.tile([P, N, PACK], BF16, name="wo_grouped", align_bytes=64)
         nc.scalar.copy(wo_grouped[:], wo_raw[:].rearrange("p i n -> p n i"))
         for g in range(GROUPS):
@@ -314,7 +313,7 @@ def tile_list_gaussian_atom_sites_kernel(
         wo_codes, wo_plane = quantize(
             wo_grouped[:].rearrange("p n i -> p (n i)"), N, "wo", f"message{last}0"
         )
-        for bank in sum_banks:
+        for bank in late_banks:
             nc.tensor.matmul_mx(
                 out=bank[:],
                 lhsT=wo_codes[:, :P].bitcast(FP8X4),
@@ -325,6 +324,9 @@ def tile_list_gaussian_atom_sites_kernel(
                 stop=True,
             )
         scatter(last, 1)
+
+        for g in range(GROUPS):
+            turn_sites(last, g)
 
         tail_banks = sum_banks + late_banks
         z_grouped = {}
@@ -378,25 +380,44 @@ def tile_list_gaussian_atom_sites_kernel(
 
         def store_group(g, engines):
             for n in range(N // P):
-                result = keep.tile([P, BANK], F32, name=f"result{g}{n}")
+                result = keep.tile(
+                    [P, BANK], F32, name=f"result{g}{n}", tag=f"message{g}{n}", align_bytes=64
+                )
                 copy_on(engines[n], result[:], tail_banks[2 * g + n][:])
                 nc.sync.dma_start(out[n * P : (n + 1) * P, g * BANK : (g + 1) * BANK], result[:])
 
+        narrow = BANK // 2
+
+        def project_half(g, half):
+            for n in range(N // P):
+                project(g, half * narrow, n, tail_banks[2 * g + half][:, n * narrow : (n + 1) * narrow])
+
+        def store_half(g, half, engine):
+            result = keep.tile([P, BANK], F32, name=f"result{g}{half}")
+            copy_on(engine, result[:], tail_banks[2 * g + half][:])
+            t0 = g * BANK + half * narrow
+            nc.sync.dma_start(
+                out[:, t0 : t0 + narrow].rearrange("(n p) t -> p n t", p=P),
+                result[:].rearrange("p (n t) -> p n t", n=N // P),
+            )
+
         for g in range(GROUPS):
-            turn_page(last, g, "scalar" if g % 2 else "vector")
-        turn_back(0, ("vector", "scalar"))
-        turn_back(1, ("vector", "scalar"))
+            turn_page(last, g, "scalar" if g == 1 else "vector")
+        turn_back(0, ("scalar", "vector"))
+        turn_back(1, ("scalar", "scalar"))
+        turn_back(2, ("scalar", "scalar"))
         quantize_z(0, 0, BANK)
-        turn_back(2, ("scalar", "vector"))
         project_group(0)
+        turn_back(3, ("scalar", "scalar"))
         quantize_z(1, 0, BANK)
-        turn_back(3, ("vector", "scalar"))
         project_group(1)
+        store_group(0, ("vector", "vector"))
         quantize_z(2, 0, BANK)
-        store_group(0, ("scalar", "scalar"))
         project_group(2)
-        store_group(1, ("vector", "scalar"))
-        quantize_z(3, 0, BANK)
-        project_group(3)
-        store_group(2, ("scalar", "vector"))
-        store_group(3, ("scalar", "vector"))
+        store_group(1, ("scalar", "scalar"))
+        for half in range(2):
+            quantize_z(3, half * narrow, narrow)
+            project_half(3, half)
+        store_group(2, ("vector", "vector"))
+        store_half(3, 0, "scalar")
+        store_half(3, 1, "scalar")

@@ -26,7 +26,7 @@ ROWS = H // P
 GROUPS = T2 // BANK
 CHUNKS = BANK // P
 COLS = BANK // 16
-PAGES = 3
+PAGES = 2
 
 
 def tile_list_gaussian_atom_sites_kernel(
@@ -60,6 +60,7 @@ def tile_list_gaussian_atom_sites_kernel(
         page_tiles = [keep.tile([P, T2], F32, name=f"pages{i}") for i in range(PAGES)]
         pages = [page_tiles[i % PAGES] for i in range(ROWS)]
         wo_raw = keep.tile([P, PACK, N], F32, name="wo_raw")
+        wo_planes = [keep.tile([P, N // 4], I32, name=f"wo_planes{k}", align_bytes=64) for k in range(2)]
         identity = keep.tile([P, P], F32, name="identity")
         warm = keep.tile([P, 8], F32, name="warm")
 
@@ -77,6 +78,7 @@ def tile_list_gaussian_atom_sites_kernel(
         nc.gpsimd.memset(wa_plane[:], 0)
         nc.gpsimd.memset(warm[:], 0.0)
         nc.gpsimd.memset(table_scales[64:, :], 0)
+        nc.gpsimd.memset(wo_planes[0][:], 0)
         nc.scalar.activation(warm[:], warm[:], ACT.Exp)
 
         nc.sync.dma_start(
@@ -194,37 +196,51 @@ def tile_list_gaussian_atom_sites_kernel(
                 stop=(a == PASSES - 1),
             )
 
-        gates = {}
-
-        def gate_of(i, h, passes=range(PASSES)):
-            for a in passes:
-                gate_pass(i, h, a)
-            square = ring.tile([P, BANK], F32, name="square", bufs=2)
-            gates[i, h] = ring.tile([P, BANK], F32, name="gate", bufs=8)
-            nc.scalar.activation(square[:], own_banks(i, h)[1][:], ACT.Square)
-            nc.scalar.activation(gates[i, h][:], square[:], ACT.Exp, scale=-1.0)
-
-        def message_of(i, h, passes=range(PASSES)):
-            for a in passes:
-                message_pass(i, h, a)
-            a_bank = own_banks(i, h)[0]
-            factor = ring.tile([P, BANK], F32, name="factor", bufs=2)
+        def new_message(i, h):
             messages[i, h] = keep.tile(
                 [P, BANK], F32, name=f"message{i}{h}", tag=f"message{i}{h}", align_bytes=64
             )
-            if (i, h) == (0, 0):
-                nc.vector.tensor_tensor(factor[:], a_bank[:], weights[h][:], MULT)
-                nc.vector.tensor_tensor(messages[i, h][:], factor[:], gates[i, h][:], MULT)
-            else:
-                raw = ring.tile([P, BANK], F32, name="raw", bufs=7)
-                nc.scalar.copy(raw[:], a_bank[:])
-                nc.gpsimd.tensor_tensor(factor[:], gates[i, h][:], weights[h][:], MULT)
-                nc.gpsimd.tensor_tensor(messages[i, h][:], factor[:], raw[:], MULT)
+            return messages[i, h]
 
-        def scatter(i, h):
+        def gate_of(i, h, pieces):
+            square = ring.tile([P, BANK], F32, name="square", bufs=2)
+            gate = ring.tile([P, BANK], F32, name="gate", bufs=8)
+            for cols in pieces:
+                nc.scalar.activation(square[:, cols], own_banks(i, h)[1][:, cols], ACT.Square)
+                nc.scalar.activation(gate[:, cols], square[:, cols], ACT.Exp, scale=-1.0)
+            return gate
+
+        def products(i, h, passes=range(PASSES)):
+            for a in passes:
+                message_pass(i, h, a)
+            raw = ring.tile([P, BANK], F32, name="raw", bufs=7)
+            nc.scalar.copy(raw[:], own_banks(i, h)[0][:])
+            factor = ring.tile([P, BANK], F32, name="factor", bufs=2)
+            nc.gpsimd.tensor_tensor(factor[:], raw[:], weights[h][:], MULT)
+            for a in passes:
+                gate_pass(i, h, a)
+            gate = gate_of(i, h, [slice(0, BANK)])
+            nc.gpsimd.tensor_tensor(new_message(i, h)[:], factor[:], gate[:], MULT)
+
+        def scatter(i, h, first=0, width=BANK):
+            col = h * COLS + first // 16
             nc.vector.tensor_copy(
-                pages[i][:].indirect(places[:, h * COLS : (h + 1) * COLS]), messages[i, h][:]
+                pages[i][:].indirect(places[:, col : col + width // 16]),
+                messages[i, h][:, first : first + width],
             )
+
+        def first_products():
+            early, late = slice(0, BANK // 2), slice(BANK // 2, BANK)
+            gate_pass(0, 0, 1)
+            message_pass(0, 0, 1)
+            gate = gate_of(0, 0, [early, late])
+            factor = keep.tile([P, BANK], F32, name="first_factor")
+            message = new_message(0, 0)
+            nc.vector.tensor_tensor(factor[:], own_banks(0, 0)[0][:], weights[0][:], MULT)
+            nc.vector.tensor_tensor(message[:, early], factor[:, early], gate[:, early], MULT)
+            nc.gpsimd.tensor_tensor(message[:, late], factor[:, late], gate[:, late], MULT)
+            scatter(0, 0, 0, BANK // 2)
+            scatter(0, 0, BANK // 2, BANK // 2)
 
         def turn(source, first, bank, g):
             for c in range(CHUNKS):
@@ -238,15 +254,16 @@ def tile_list_gaussian_atom_sites_kernel(
                     stop=(not first and c == CHUNKS - 1),
                 )
 
-        z_rows = [
-            keep.tile(
+        z_rows = {
+            (s, j): keep.tile(
                 [P, 2, CHUNKS, 2 * P],
                 BF16,
-                name=f"z_rows{g}",
-                tag=f"table_words{g}" if g < PASSES else f"z_rows{g}",
+                name=f"z_rows{s}{j}",
+                tag=f"table_words{j}" if s == 0 else f"z_rows{j}",
             )
-            for g in range(GROUPS)
-        ]
+            for s in range(2)
+            for j in range(2)
+        }
 
         def copy_on(engine, dst, src):
             if engine == "vector":
@@ -255,17 +272,18 @@ def tile_list_gaussian_atom_sites_kernel(
                 nc.scalar.copy(dst, src)
 
         def round_z(i, g, engine, into):
+            at = P * ((g % 2) ^ (i // 2)) + 64 * (i % 2)
             copy_on(
                 engine,
-                z_rows[g][:, :, :, 64 * i : 64 * (i + 1)].rearrange("p u c (m e) -> p u c m e", e=2),
+                z_rows[i // 2, g // 2][:, :, :, at : at + 64].rearrange("p u c (m e) -> p u c m e", e=2),
                 into[g][:].rearrange("p (c m u e) -> p u c m e", c=CHUNKS, u=2, e=2),
             )
 
         last = ROWS - 1
-        late_banks = [banks[1], banks[3], banks[0], banks[2]]
+        freed_banks = [banks[1], banks[0], banks[3], banks[2]]
 
         def sums_of(i):
-            return late_banks if i == last else sum_banks
+            return freed_banks if i == 2 else sum_banks
 
         def turn_sites(i, g):
             turn(states[i][:], True, sums_of(i)[g], g)
@@ -274,17 +292,36 @@ def tile_list_gaussian_atom_sites_kernel(
             turn(pages[i][:], False, sums_of(i)[g], g)
             round_z(i, g, engine, sums_of(i))
 
-        def products(i, h, passes=range(PASSES)):
-            gate_of(i, h, passes)
-            message_of(i, h, passes)
+        z_grouped = [
+            keep.tile([P, BANK, PACK], BF16, name=f"z_grouped{g}", tag=f"spent{g}", align_bytes=64)
+            for g in range(GROUPS)
+        ]
+
+        def turn_back(s, j, half, bank):
+            words = z_rows[s, j][:].bitcast(F32)
+            for c2 in range(2):
+                for u in range(2):
+                    col = (2 * c2 + u) * P
+                    nc.tensor.transpose(
+                        bank[:, col : col + P], words[:, u, 2 * half + c2, :], identity[:]
+                    )
+
+        def weave(s, g, half, bank, engine):
+            rows = slice(64 * ((g % 2) ^ s), 64 * ((g % 2) ^ s) + 64)
+            grouped_words = z_grouped[g][:].rearrange("p t i -> p (t i)").bitcast(F32)
+            copy_on(
+                engine,
+                grouped_words[rows, half * BANK : (half + 1) * BANK].rearrange(
+                    "p (c t u) -> p c t u", c=2, u=2
+                ),
+                bank[rows, :].rearrange("p (c u t) -> p c t u", c=2, u=2),
+            )
 
         for i in range(2):
             for h in range(HALVES):
                 gate_pass(i, h, 0)
                 message_pass(i, h, 0)
-        gate_of(0, 0, [1])
-        message_of(0, 0, [1])
-        scatter(0, 0)
+        first_products()
         products(0, 1, [1])
         next_wg(2)
         scatter(0, 1)
@@ -293,131 +330,107 @@ def tile_list_gaussian_atom_sites_kernel(
         scatter(1, 0)
         products(1, 1, [1])
         scatter(1, 1)
-        for i in range(2, ROWS):
-            for h in range(HALVES):
-                products(i, h)
-            if i == 2:
-                for g in range(GROUPS):
-                    turn_sites(0, g)
+        for h in range(HALVES):
+            products(2, h)
+        for g in range(GROUPS):
+            turn_sites(0, g)
+        for g in range(GROUPS):
+            turn_page(0, g)
+        for h in range(HALVES):
+            scatter(2, h)
+            products(last, h)
+        for i in (1, 2):
             for g in range(GROUPS):
-                turn_page(i - 2, g)
-            for g in range(GROUPS):
-                turn_sites(i - 1, g)
-            scatter(i, 0)
-            if i < last:
-                scatter(i, 1)
+                turn_sites(i, g)
+        for g in range(GROUPS):
+            turn_page(1, g)
+        scatter(last, 0)
         wo_grouped = keep.tile([P, N, PACK], BF16, name="wo_grouped", align_bytes=64)
         nc.scalar.copy(wo_grouped[:], wo_raw[:].rearrange("p i n -> p n i"))
+        for j in range(2):
+            for half in range(2):
+                bank = sum_banks[2 * j + half]
+                turn_back(0, j, half, bank)
+                for g in (2 * j, 2 * j + 1):
+                    weave(0, g, half, bank, "scalar")
         for g in range(GROUPS):
             turn_page(last - 1, g)
-        wo_codes, wo_plane = quantize(
-            wo_grouped[:].rearrange("p n i -> p (n i)"), N, "wo", f"message{last}0"
+        wo_codes = [
+            keep.tile([P, N], U32, name="wo_codes0", tag=f"message{last}0", align_bytes=64),
+            keep.tile([P, N], U32, name="wo_codes1", align_bytes=64),
+        ]
+        nc.vector.quantize_mx(
+            out=wo_codes[0][:].bitcast(FP8X4),
+            scales=wo_planes[0][:].bitcast(U8),
+            in_=wo_grouped[:].rearrange("p n i -> p (n i)"),
         )
-        for bank in late_banks:
+        for low in (0, 64):
+            there, here = slice(low, low + 64), slice(64 - low, P - low)
+            nc.sync.dma_start(wo_codes[1][there, :].bitcast(I32), wo_codes[0][here, :].bitcast(I32))
+            nc.sync.dma_start(wo_planes[1][there, :], wo_planes[0][here, :])
+        for bank in sum_banks:
             nc.tensor.matmul_mx(
                 out=bank[:],
-                lhsT=wo_codes[:, :P].bitcast(FP8X4),
-                lhsT_scale=wo_plane[:, :P],
+                lhsT=wo_codes[0][:, :P].bitcast(FP8X4),
+                lhsT_scale=wo_planes[0][:].bitcast(U8)[:, :P],
                 rhs=v_codes[0, 0].bitcast(FP8X4),
                 rhs_scale=v_plane[0, 0],
                 start=True,
                 stop=True,
             )
         scatter(last, 1)
-
         for g in range(GROUPS):
             turn_sites(last, g)
 
-        tail_banks = sum_banks + late_banks
-        z_grouped = {}
-
-        def turn_back(g, engines):
-            z_grouped[g] = keep.tile(
-                [P, BANK, PACK], BF16, name=f"z_grouped{g}", tag=f"spent{g}", align_bytes=64
-            )
-            words = z_rows[g][:].bitcast(F32)
-            grouped_words = z_grouped[g][:].rearrange("p t i -> p (t i)").bitcast(F32)
-            for half in range(2):
-                bank = tail_banks[2 * g + half]
-                for c2 in range(2):
-                    for u in range(2):
-                        col = (2 * c2 + u) * P
-                        nc.tensor.transpose(
-                            bank[:, col : col + P], words[:, u, 2 * half + c2, :], identity[:]
-                        )
-                copy_on(
-                    engines[half],
-                    grouped_words[:, half * BANK : (half + 1) * BANK].rearrange(
-                        "p (c t u) -> p c t u", c=2, u=2
-                    ),
-                    bank[:].rearrange("p (c u t) -> p c t u", c=2, u=2),
-                )
-
+        out_banks = sum_banks + freed_banks
         z_q = {}
 
-        def quantize_z(g, first, width):
-            z_q[g, first] = quantize(
-                z_grouped[g][:, first : first + width, :].rearrange("p t i -> p (t i)"),
-                width,
-                f"z{g}{first}",
-            )
+        def quantize_z(g):
+            z_q[g] = quantize(z_grouped[g][:].rearrange("p t i -> p (t i)"), BANK, f"z{g}")
 
-        def project(g, first, n, target):
-            z_codes, z_plane = z_q[g, first]
-            nc.tensor.matmul_mx(
-                out=target,
-                lhsT=wo_codes[:, n * P : (n + 1) * P].bitcast(FP8X4),
-                lhsT_scale=wo_plane[:, n * P : (n + 1) * P],
-                rhs=z_codes[:].bitcast(FP8X4),
-                rhs_scale=z_plane[:],
-                start=True,
-                stop=True,
-            )
-
-        def project_group(g):
+        def project(g):
+            z_codes, z_plane = z_q[g]
             for n in range(N // P):
-                project(g, 0, n, tail_banks[2 * g + n][:])
-
-        def store_group(g, engines):
-            for n in range(N // P):
-                result = keep.tile(
-                    [P, BANK], F32, name=f"result{g}{n}", tag=f"message{g}{n}", align_bytes=64
+                nc.tensor.matmul_mx(
+                    out=out_banks[2 * g + n][:],
+                    lhsT=wo_codes[g % 2][:, n * P : (n + 1) * P].bitcast(FP8X4),
+                    lhsT_scale=wo_planes[g % 2][:].bitcast(U8)[:, n * P : (n + 1) * P],
+                    rhs=z_codes[:].bitcast(FP8X4),
+                    rhs_scale=z_plane[:],
+                    start=True,
+                    stop=True,
                 )
-                copy_on(engines[n], result[:], tail_banks[2 * g + n][:])
-                nc.sync.dma_start(out[n * P : (n + 1) * P, g * BANK : (g + 1) * BANK], result[:])
 
-        narrow = BANK // 2
-
-        def project_half(g, half):
-            for n in range(N // P):
-                project(g, half * narrow, n, tail_banks[2 * g + half][:, n * narrow : (n + 1) * narrow])
-
-        def store_half(g, half, engine):
-            result = keep.tile([P, BANK], F32, name=f"result{g}{half}")
-            copy_on(engine, result[:], tail_banks[2 * g + half][:])
-            t0 = g * BANK + half * narrow
-            nc.sync.dma_start(
-                out[:, t0 : t0 + narrow].rearrange("(n p) t -> p n t", p=P),
-                result[:].rearrange("p (n t) -> p n t", n=N // P),
+        def store(g, n, engine):
+            result = keep.tile(
+                [P, BANK], F32, name=f"result{g}{n}", tag=f"message{g}{n}" if g < last else f"result{n}", align_bytes=64
             )
+            copy_on(engine, result[:], out_banks[2 * g + n][:])
+            nc.sync.dma_start(out[n * P : (n + 1) * P, g * BANK : (g + 1) * BANK], result[:])
 
         for g in range(GROUPS):
-            turn_page(last, g, "scalar" if g == 1 else "vector")
-        turn_back(0, ("scalar", "vector"))
-        turn_back(1, ("scalar", "scalar"))
-        turn_back(2, ("scalar", "scalar"))
-        quantize_z(0, 0, BANK)
-        project_group(0)
-        turn_back(3, ("scalar", "scalar"))
-        quantize_z(1, 0, BANK)
-        project_group(1)
-        store_group(0, ("vector", "vector"))
-        quantize_z(2, 0, BANK)
-        project_group(2)
-        store_group(1, ("scalar", "scalar"))
+            turn_page(last, g, "scalar" if g % 2 else "vector")
+        for j in range(2):
+            for half in range(2):
+                turn_back(1, j, half, freed_banks[2 * j + half])
+        for g in range(2):
+            weave(1, g, 0, freed_banks[0], "vector")
+            weave(1, g, 1, freed_banks[1], "scalar")
         for half in range(2):
-            quantize_z(3, half * narrow, narrow)
-            project_half(3, half)
-        store_group(2, ("vector", "vector"))
-        store_half(3, 0, "scalar")
-        store_half(3, 1, "scalar")
+            weave(1, 2, half, freed_banks[2 + half], "scalar")
+        for g in range(2):
+            quantize_z(g)
+            project(g)
+        weave(1, last, 0, freed_banks[2], "vector")
+        quantize_z(2)
+        weave(1, last, 1, freed_banks[3], "vector")
+        project(2)
+        for g in range(2):
+            for n in range(N // P):
+                store(g, n, "scalar")
+        quantize_z(last)
+        project(last)
+        store(2, 0, "scalar")
+        store(2, 1, "vector")
+        store(last, 0, "vector")
+        store(last, 1, "scalar")

@@ -50,11 +50,13 @@ def tile_list_gaussian_atom_sites_kernel(
         ]
         wa_codes = keep.tile([P, PASSES, 2 * H // 4], I32, name="wa_codes", align_bytes=64)
         wa_plane = keep.tile([P, PASSES, H // 4], I32, name="wa_plane", align_bytes=64)
-        wg_first = [keep.tile([P, PACK, 2 * P], F32, name=f"wg_first{a}") for a in range(PASSES)]
-        wg_rest = [
-            keep.tile([P, PACK, H - 2 * P], F32, name=f"wg_rest{a}", tag=f"spent{a}", align_bytes=64)
+        wg_pair = keep.tile([P, PACK, 2 * P], F32, name="wg_pair")
+        wg_second = [keep.tile([P, PACK, P], F32, name=f"wg_second{i}") for i in range(2)]
+        wg_rest = {
+            (i, a): keep.tile([P, PACK, P], F32, name=f"wg_rest{i}{a}", tag=f"spent{2 * (i - 2) + a}", align_bytes=64)
+            for i in range(2, ROWS)
             for a in range(PASSES)
-        ]
+        }
         weights = [keep.tile([P, BANK], F32, name=f"weights{h}") for h in range(HALVES)]
         states = [keep.tile([P, T2], F32, name=f"states{i}") for i in range(ROWS)]
         page_tiles = [keep.tile([P, T2], F32, name=f"pages{i}") for i in range(PAGES)]
@@ -62,7 +64,6 @@ def tile_list_gaussian_atom_sites_kernel(
         wo_raw = keep.tile([P, PACK, N], F32, name="wo_raw")
         wo_planes = [keep.tile([P, N // 4], I32, name=f"wo_planes{k}", align_bytes=64) for k in range(2)]
         identity = keep.tile([P, P], F32, name="identity")
-        warm = keep.tile([P, 8], F32, name="warm")
 
         def wg_rows(a):
             return wg[a * P * PACK : (a + 1) * P * PACK, :].rearrange("(p i) r -> p i r", i=PACK)
@@ -76,24 +77,22 @@ def tile_list_gaussian_atom_sites_kernel(
         for a in range(PASSES):
             nc.vector.memset(v_planes[a][:], 0)
         nc.gpsimd.memset(wa_plane[:], 0)
-        nc.gpsimd.memset(warm[:], 0.0)
         nc.gpsimd.memset(table_scales[64:, :], 0)
         nc.gpsimd.memset(wo_planes[0][:], 0)
-        nc.scalar.activation(warm[:], warm[:], ACT.Exp)
 
         nc.sync.dma_start(
             table_scales[:32, :], tab_scales.rearrange("a q t -> (a q) t").bitcast(I32)
         )
         nc.sync.dma_start(atoms[:], offs)
-        load_words(0)
         for r in range(4):
             nc.sync.dma_start(
                 wa_plane[r:P:32, :, :],
                 wa_scales[:, r:16:4, :].rearrange("a q c -> q a c").bitcast(I32),
             )
         nc.sync.dma_start(wa_codes[:], wa_words.rearrange("a p b -> p a b").bitcast(I32))
-        for a in range(PASSES):
-            nc.sync.dma_start(wg_first[a][:], wg_rows(a)[:, :, : 2 * P])
+        load_words(0)
+        nc.sync.dma_start(wg_pair[:], wg_rows(0)[:, :, : 2 * P])
+        nc.sync.dma_start(wg_second[0][:], wg_rows(1)[:, :, :P])
         v_codes, v_plane = {}, {}
 
         picked_scales = keep.tile([P, S // 4], I32, name="picked_scales")
@@ -105,19 +104,20 @@ def tile_list_gaussian_atom_sites_kernel(
         def move_scales(a, r):
             nc.sync.dma_start(v_planes[a][r:P:32, :], picked_scales[16 * a + r : 16 * (a + 1) : 4, :])
 
-        for a, r in moves[:5]:
+        for a, r in moves[:4]:
             move_scales(a, r)
         load_words(1)
-        for a, r in moves[5:]:
+        for a, r in moves[4:]:
             move_scales(a, r)
         for a in range(PASSES):
             for h in range(HALVES):
                 v_plane[a, h] = v_planes[a][:].bitcast(U8)[:, h * BANK : (h + 1) * BANK]
-        nc.sync.dma_start(places[:], offs2)
         nc.sync.dma_start(weights[0][:], wgs[:, :BANK])
-        for a in range(PASSES):
-            nc.sync.dma_start(wg_rest[a][:], wg_rows(a)[:, :, 2 * P :])
+        nc.sync.dma_start(places[:], offs2)
+        nc.sync.dma_start(wg_second[1][:], wg_rows(1)[:, :, P : 2 * P])
         nc.sync.dma_start(weights[1][:], wgs[:, BANK:])
+        for i, a in wg_rest:
+            nc.sync.dma_start(wg_rest[i, a][:], wg_rows(a)[:, :, i * P : (i + 1) * P])
         nc.sync.dma_start(states[0][:], sites[:P, :])
         nc.sync.dma_start(wo_raw[:], wo.rearrange("(p i) n -> p i n", i=PACK))
         for i in range(1, ROWS):
@@ -128,12 +128,14 @@ def tile_list_gaussian_atom_sites_kernel(
             for g in range(GROUPS):
                 nc.vector.memset(page[:, g * BANK : (g + 1) * BANK].bitcast(I32), 0)
 
-        def gather_words(a, h, picked):
+        def gather_words(a, h, picked, pieces=1):
             v_codes[a, h] = picked[:, a, h * BANK : (h + 1) * BANK]
-            nc.vector.tensor_copy(
-                v_codes[a, h],
-                table_words[a][:].bitcast(U32).indirect(atoms[:, h * COLS : (h + 1) * COLS]),
-            )
+            width = BANK // pieces
+            for first in range(h * BANK, (h + 1) * BANK, width):
+                nc.vector.tensor_copy(
+                    picked[:, a, first : first + width],
+                    table_words[a][:].bitcast(U32).indirect(atoms[:, first // 16 : (first + width) // 16]),
+                )
 
         def quantize(grouped, width, name, tag=None):
             codes = keep.tile(
@@ -145,25 +147,26 @@ def tile_list_gaussian_atom_sites_kernel(
 
         wg_q = {}
 
-        def quantize_wg(i, raw):
-            grouped = keep.tile([P, PASSES, P, PACK], BF16, name=f"wg_grouped{i}", align_bytes=64)
-            for a in range(PASSES):
-                nc.scalar.copy(grouped[:, a, :, :], raw[a].rearrange("p i r -> p r i"))
-            codes, plane = quantize(
-                grouped[:].rearrange("p a r i -> p (a r i)"), PASSES * P, f"wg{i}"
-            )
-            wg_q[i] = (codes[:], plane[:])
+        def quantize_wg(keys, raws):
+            name = "wg" + "".join(f"{i}{a}" for i, a in keys)
+            grouped = keep.tile([P, len(keys) * P, PACK], BF16, name=f"{name}_grouped", align_bytes=64)
+            width = len(keys) * P // len(raws)
+            for n, raw in enumerate(raws):
+                nc.scalar.copy(grouped[:, n * width : (n + 1) * width, :], raw[:].rearrange("p i r -> p r i"))
+            codes, plane = quantize(grouped[:].rearrange("p r i -> p (r i)"), len(keys) * P, name)
+            for n, key in enumerate(keys):
+                wg_q[key] = (codes[:, n * P : (n + 1) * P], plane[:, n * P : (n + 1) * P])
 
         def next_wg(i):
-            quantize_wg(i, [wg_rest[a][:, :, (i - 2) * P : (i - 1) * P] for a in range(PASSES)])
+            quantize_wg([(i, a) for a in range(PASSES)], [wg_rest[i, a] for a in range(PASSES)])
 
         picked = keep.tile([P, PASSES, S], U32, name="picked", align_bytes=64)
         for h in range(HALVES):
             gather_words(0, h, picked)
-        for i in range(2):
-            quantize_wg(i, [wg_first[a][:, :, i * P : (i + 1) * P] for a in range(PASSES)])
-        for h in range(HALVES):
-            gather_words(1, h, picked)
+        quantize_wg([(0, 0), (1, 0)], [wg_pair])
+        quantize_wg([(0, 1)], [wg_second[0]])
+        gather_words(1, 0, picked, pieces=2)
+        gather_words(1, 1, picked)
 
         product_banks = banks[:4]
         sum_banks = banks[4:]
@@ -174,11 +177,11 @@ def tile_list_gaussian_atom_sites_kernel(
             return own[2 * h], own[2 * h + 1]
 
         def gate_pass(i, h, a):
-            wg_codes, wg_plane = wg_q[i]
+            wg_codes, wg_plane = wg_q[i, a]
             nc.tensor.matmul_mx(
                 out=own_banks(i, h)[1][:],
-                lhsT=wg_codes[:, a * P : (a + 1) * P].bitcast(FP8X4),
-                lhsT_scale=wg_plane[:, a * P : (a + 1) * P],
+                lhsT=wg_codes.bitcast(FP8X4),
+                lhsT_scale=wg_plane,
                 rhs=v_codes[a, h].bitcast(FP8X4),
                 rhs_scale=v_plane[a, h],
                 start=(a == 0),
@@ -196,15 +199,22 @@ def tile_list_gaussian_atom_sites_kernel(
                 stop=(a == PASSES - 1),
             )
 
+        whole_messages = {i: keep.tile([P, S], F32, name=f"message{i}") for i in (2,)}
+
         def new_message(i, h):
+            if i in whole_messages:
+                return whole_messages[i][:, h * BANK : (h + 1) * BANK]
             messages[i, h] = keep.tile(
                 [P, BANK], F32, name=f"message{i}{h}", tag=f"message{i}{h}", align_bytes=64
             )
-            return messages[i, h]
+            return messages[i, h][:]
+
+        def scatter_whole(i):
+            nc.vector.tensor_copy(pages[i][:].indirect(places[:]), whole_messages[i][:])
 
         def gate_of(i, h, pieces):
             square = ring.tile([P, BANK], F32, name="square", bufs=2)
-            gate = ring.tile([P, BANK], F32, name="gate", bufs=8)
+            gate = ring.tile([P, BANK], F32, name="gate", bufs=4)
             for cols in pieces:
                 nc.scalar.activation(square[:, cols], own_banks(i, h)[1][:, cols], ACT.Square)
                 nc.scalar.activation(gate[:, cols], square[:, cols], ACT.Exp, scale=-1.0)
@@ -213,14 +223,14 @@ def tile_list_gaussian_atom_sites_kernel(
         def products(i, h, passes=range(PASSES)):
             for a in passes:
                 message_pass(i, h, a)
-            raw = ring.tile([P, BANK], F32, name="raw", bufs=7)
+            raw = ring.tile([P, BANK], F32, name="raw", bufs=4)
             nc.scalar.copy(raw[:], own_banks(i, h)[0][:])
             factor = ring.tile([P, BANK], F32, name="factor", bufs=2)
             nc.gpsimd.tensor_tensor(factor[:], raw[:], weights[h][:], MULT)
             for a in passes:
                 gate_pass(i, h, a)
             gate = gate_of(i, h, [slice(0, BANK)])
-            nc.gpsimd.tensor_tensor(new_message(i, h)[:], factor[:], gate[:], MULT)
+            nc.gpsimd.tensor_tensor(new_message(i, h), factor[:], gate[:], MULT)
 
         def scatter(i, h, first=0, width=BANK):
             col = h * COLS + first // 16
@@ -229,18 +239,46 @@ def tile_list_gaussian_atom_sites_kernel(
                 messages[i, h][:, first : first + width],
             )
 
+        QUARTER = BANK // 2
+
+        def quarter_passes(q, a):
+            cols = slice(q * QUARTER, (q + 1) * QUARTER)
+            wg_codes, wg_plane = wg_q[0, a]
+            nc.tensor.matmul_mx(
+                out=banks[q][:, :QUARTER],
+                lhsT=wa_codes[:, a, :].bitcast(U8)[:, : 2 * P].bitcast(FP4X4),
+                lhsT_scale=wa_plane[:, a, :].bitcast(U8)[:, :P],
+                rhs=v_codes[a, 0][:, cols].bitcast(FP8X4),
+                rhs_scale=v_plane[a, 0][:, cols],
+                start=(a == 0),
+                stop=False,
+            )
+            nc.tensor.matmul_mx(
+                out=banks[q][:, QUARTER:],
+                lhsT=wg_codes.bitcast(FP8X4),
+                lhsT_scale=wg_plane,
+                rhs=v_codes[a, 0][:, cols].bitcast(FP8X4),
+                rhs_scale=v_plane[a, 0][:, cols],
+                start=False,
+                stop=(a == PASSES - 1),
+            )
+
         def first_products():
-            early, late = slice(0, BANK // 2), slice(BANK // 2, BANK)
-            gate_pass(0, 0, 1)
-            message_pass(0, 0, 1)
-            gate = gate_of(0, 0, [early, late])
-            factor = keep.tile([P, BANK], F32, name="first_factor")
             message = new_message(0, 0)
-            nc.vector.tensor_tensor(factor[:], own_banks(0, 0)[0][:], weights[0][:], MULT)
-            nc.vector.tensor_tensor(message[:, early], factor[:, early], gate[:, early], MULT)
-            nc.gpsimd.tensor_tensor(message[:, late], factor[:, late], gate[:, late], MULT)
-            scatter(0, 0, 0, BANK // 2)
-            scatter(0, 0, BANK // 2, BANK // 2)
+            for q in range(2):
+                cols = slice(q * QUARTER, (q + 1) * QUARTER)
+                quarter_passes(q, 1)
+                raw, square, gate, factor = [
+                    keep.tile([P, QUARTER], F32, name=f"first_{name}{q}")
+                    for name in ("raw", "square", "gate", "factor")
+                ]
+                nc.scalar.copy(raw[:], banks[q][:, :QUARTER])
+                nc.gpsimd.tensor_tensor(factor[:], raw[:], weights[0][:, cols], MULT)
+                nc.scalar.activation(square[:], banks[q][:, QUARTER:], ACT.Square)
+                nc.scalar.activation(gate[:], square[:], ACT.Exp, scale=-1.0)
+                engine = nc.gpsimd if q else nc.vector
+                engine.tensor_tensor(message[:, cols], factor[:], gate[:], MULT)
+                scatter(0, 0, q * QUARTER, QUARTER)
 
         def turn(source, first, bank, g):
             for c in range(CHUNKS):
@@ -317,17 +355,19 @@ def tile_list_gaussian_atom_sites_kernel(
                 bank[rows, :].rearrange("p (c u t) -> p c t u", c=2, u=2),
             )
 
-        for i in range(2):
-            for h in range(HALVES):
-                gate_pass(i, h, 0)
-                message_pass(i, h, 0)
+        for q in range(2):
+            quarter_passes(q, 0)
+        for i, h in ((0, 1), (1, 0), (1, 1)):
+            gate_pass(i, h, 0)
+            message_pass(i, h, 0)
         first_products()
+        quantize_wg([(1, 1)], [wg_second[1]])
         products(0, 1, [1])
-        next_wg(2)
         scatter(0, 1)
+        next_wg(2)
         products(1, 0, [1])
-        next_wg(3)
         scatter(1, 0)
+        next_wg(3)
         products(1, 1, [1])
         scatter(1, 1)
         for h in range(HALVES):
@@ -336,14 +376,15 @@ def tile_list_gaussian_atom_sites_kernel(
             turn_sites(0, g)
         for g in range(GROUPS):
             turn_page(0, g)
+        scatter_whole(2)
         for h in range(HALVES):
-            scatter(2, h)
             products(last, h)
-        for i in (1, 2):
-            for g in range(GROUPS):
-                turn_sites(i, g)
+        for g in range(GROUPS):
+            turn_sites(1, g)
         for g in range(GROUPS):
             turn_page(1, g)
+        for g in range(GROUPS):
+            turn_sites(2, g)
         scatter(last, 0)
         wo_grouped = keep.tile([P, N, PACK], BF16, name="wo_grouped", align_bytes=64)
         nc.scalar.copy(wo_grouped[:], wo_raw[:].rearrange("p i n -> p n i"))
@@ -368,16 +409,6 @@ def tile_list_gaussian_atom_sites_kernel(
             there, here = slice(low, low + 64), slice(64 - low, P - low)
             nc.sync.dma_start(wo_codes[1][there, :].bitcast(I32), wo_codes[0][here, :].bitcast(I32))
             nc.sync.dma_start(wo_planes[1][there, :], wo_planes[0][here, :])
-        for bank in sum_banks:
-            nc.tensor.matmul_mx(
-                out=bank[:],
-                lhsT=wo_codes[0][:, :P].bitcast(FP8X4),
-                lhsT_scale=wo_planes[0][:].bitcast(U8)[:, :P],
-                rhs=v_codes[0, 0].bitcast(FP8X4),
-                rhs_scale=v_plane[0, 0],
-                start=True,
-                stop=True,
-            )
         scatter(last, 1)
         for g in range(GROUPS):
             turn_sites(last, g)
@@ -403,7 +434,7 @@ def tile_list_gaussian_atom_sites_kernel(
 
         def store(g, n, engine):
             result = keep.tile(
-                [P, BANK], F32, name=f"result{g}{n}", tag=f"message{g}{n}" if g < last else f"result{n}", align_bytes=64
+                [P, BANK], F32, name=f"result{g}{n}", tag=f"message{g}{n}" if g < 2 else f"result{g}{n}", align_bytes=64
             )
             copy_on(engine, result[:], out_banks[2 * g + n][:])
             nc.sync.dma_start(out[n * P : (n + 1) * P, g * BANK : (g + 1) * BANK], result[:])

@@ -409,6 +409,16 @@ def tile_list_gaussian_atom_sites_kernel(
             there, here = slice(low, low + 64), slice(64 - low, P - low)
             nc.sync.dma_start(wo_codes[1][there, :].bitcast(I32), wo_codes[0][here, :].bitcast(I32))
             nc.sync.dma_start(wo_planes[1][there, :], wo_planes[0][here, :])
+        for bank in sum_banks:
+            nc.tensor.matmul_mx(
+                out=bank[:],
+                lhsT=wo_codes[0][:, :P].bitcast(FP8X4),
+                lhsT_scale=wo_planes[0][:].bitcast(U8)[:, :P],
+                rhs=v_codes[0, 0].bitcast(FP8X4),
+                rhs_scale=v_plane[0, 0],
+                start=True,
+                stop=True,
+            )
         scatter(last, 1)
         for g in range(GROUPS):
             turn_sites(last, g)

@@ -199,18 +199,11 @@ def tile_list_gaussian_atom_sites_kernel(
                 stop=(a == PASSES - 1),
             )
 
-        whole_messages = {i: keep.tile([P, S], F32, name=f"message{i}") for i in (2,)}
-
         def new_message(i, h):
-            if i in whole_messages:
-                return whole_messages[i][:, h * BANK : (h + 1) * BANK]
             messages[i, h] = keep.tile(
                 [P, BANK], F32, name=f"message{i}{h}", tag=f"message{i}{h}", align_bytes=64
             )
             return messages[i, h][:]
-
-        def scatter_whole(i):
-            nc.vector.tensor_copy(pages[i][:].indirect(places[:]), whole_messages[i][:])
 
         def gate_of(i, h, pieces):
             square = ring.tile([P, BANK], F32, name="square", bufs=2)
@@ -231,6 +224,26 @@ def tile_list_gaussian_atom_sites_kernel(
                 gate_pass(i, h, a)
             gate = gate_of(i, h, [slice(0, BANK)])
             nc.gpsimd.tensor_tensor(new_message(i, h), factor[:], gate[:], MULT)
+
+        def last_products():
+            i, h = ROWS - 1, HALVES - 1
+            for a in range(PASSES):
+                message_pass(i, h, a)
+            raw = ring.tile([P, BANK], F32, name="raw", bufs=4)
+            nc.scalar.copy(raw[:], own_banks(i, h)[0][:])
+            for a in range(PASSES):
+                gate_pass(i, h, a)
+            gate = gate_of(i, h, [slice(0, BANK)])
+            nc.gpsimd.tensor_tensor(new_message(i, h), raw[:], gate[:], MULT)
+
+        def last_scatter():
+            i, h = ROWS - 1, HALVES - 1
+            nc.vector.tensor_tensor(
+                pages[i][:].indirect(places[:, h * COLS : (h + 1) * COLS]),
+                messages[i, h][:],
+                weights[h][:],
+                MULT,
+            )
 
         def scatter(i, h, first=0, width=BANK):
             col = h * COLS + first // 16
@@ -376,9 +389,10 @@ def tile_list_gaussian_atom_sites_kernel(
             turn_sites(0, g)
         for g in range(GROUPS):
             turn_page(0, g)
-        scatter_whole(2)
-        for h in range(HALVES):
-            products(last, h)
+        scatter(2, 0)
+        products(last, 0)
+        scatter(2, 1)
+        last_products()
         for g in range(GROUPS):
             turn_sites(1, g)
         for g in range(GROUPS):
@@ -419,7 +433,7 @@ def tile_list_gaussian_atom_sites_kernel(
                 start=True,
                 stop=True,
             )
-        scatter(last, 1)
+        last_scatter()
         for g in range(GROUPS):
             turn_sites(last, g)
 
@@ -444,7 +458,7 @@ def tile_list_gaussian_atom_sites_kernel(
 
         def store(g, n, engine):
             result = keep.tile(
-                [P, BANK], F32, name=f"result{g}{n}", tag=f"message{g}{n}" if g < 2 else f"result{g}{n}", align_bytes=64
+                [P, BANK], F32, name=f"result{g}{n}", tag=f"message{g}{n}" if g < last else f"result{n}", align_bytes=64
             )
             copy_on(engine, result[:], out_banks[2 * g + n][:])
             nc.sync.dma_start(out[n * P : (n + 1) * P, g * BANK : (g + 1) * BANK], result[:])

@@ -173,6 +173,8 @@ def tile_list_gaussian_atom_sites_kernel(
         messages = {}
 
         def own_banks(i, h):
+            if (i, h) == (ROWS - 1, HALVES - 1):
+                return sum_banks[0], sum_banks[1]
             own = sum_banks if i == 1 else product_banks
             return own[2 * h], own[2 * h + 1]
 
@@ -392,10 +394,12 @@ def tile_list_gaussian_atom_sites_kernel(
         scatter(2, 0)
         products(last, 0)
         scatter(2, 1)
-        last_products()
         for g in range(GROUPS):
             turn_sites(1, g)
-        for g in range(GROUPS):
+        for g in range(2):
+            turn_page(1, g)
+        last_products()
+        for g in range(2, GROUPS):
             turn_page(1, g)
         for g in range(GROUPS):
             turn_sites(2, g)

from contextlib import ExitStack

import concourse.mybir as mybir
from concourse.masks import make_identity

K, T, S, T2, H, N = 1024, 4096, 1024, 2048, 512, 256
FLOPS = 2 * (2 * K * H * S + H * N * T2)

F32 = mybir.dt.float32
BF16 = mybir.dt.bfloat16
I32 = mybir.dt.int32
U32 = mybir.dt.uint32
U16 = mybir.dt.uint16
U8 = mybir.dt.uint8
FP8X4 = mybir.dt.float8_e4m3fn_x4
FP4X4 = mybir.dt.float4_e2m1fn_x4
ACT = mybir.ActivationFunctionType
MULT = mybir.AluOpType.mult

P = 128
PACK = 4
PASSES = K // (P * PACK)
BANK = 512
HALVES = S // BANK
ROWS = H // P
GROUPS = T2 // BANK
CHUNKS = BANK // P
COLS = BANK // 16
PAGES = 2


def tile_list_gaussian_atom_sites_kernel(
    tc, tab_words, tab_scales, offs, wa_words, wa_scales, wg, wgs, offs2, sites, wo, out
):
    nc = tc.nc
    with ExitStack() as ctx:
        lists = ctx.enter_context(tc.tile_pool(name="lists", bufs=1))
        keep = ctx.enter_context(tc.tile_pool(name="keep", bufs=1))
        ring = ctx.enter_context(tc.tile_pool(name="ring", bufs=3))
        psum = ctx.enter_context(tc.psum_pool(name="psum", bufs=1))

        banks = [psum.tile([P, BANK], F32, name=f"bank{b}") for b in range(8)]

        atoms = lists.tile([P, S // 16], U16, name="atoms")
        places = lists.tile([P, S // 16], U16, name="places")
        table_words = [keep.tile([P, T], I32, name=f"table_words{a}", tag=f"table_words{a}") for a in range(PASSES)]
        table_scales = keep.tile([P, T // 4], I32, name="table_scales")
        v_planes = [
            keep.tile([P, S // 4], I32, name=f"v_planes{a}", align_bytes=64) for a in range(PASSES)
        ]
        wa_codes = keep.tile([P, PASSES, 2 * H // 4], I32, name="wa_codes", align_bytes=64)
        wa_plane = keep.tile([P, PASSES, H // 4], I32, name="wa_plane", align_bytes=64)
        wg_pair = keep.tile([P, PACK, 2 * P], F32, name="wg_pair")
        wg_second = [keep.tile([P, PACK, P], F32, name=f"wg_second{i}") for i in range(2)]
        wg_rest = {
            (i, a): keep.tile([P, PACK, P], F32, name=f"wg_rest{i}{a}", tag=f"spent{2 * (i - 2) + a}", align_bytes=64)
            for i in range(2, ROWS)
            for a in range(PASSES)
        }
        weights = [keep.tile([P, BANK], F32, name=f"weights{h}") for h in range(HALVES)]
        states = [keep.tile([P, T2], F32, name=f"states{i}") for i in range(ROWS)]
        page_tiles = [keep.tile([P, T2], F32, name=f"pages{i}") for i in range(PAGES)]
        pages = [page_tiles[i % PAGES] for i in range(ROWS)]
        wo_raw = keep.tile([P, PACK, N], F32, name="wo_raw")
        wo_planes = [keep.tile([P, N // 4], I32, name=f"wo_planes{k}", align_bytes=64) for k in range(2)]
        identity = keep.tile([P, P], F32, name="identity")

        def wg_rows(a):
            return wg[a * P * PACK : (a + 1) * P * PACK, :].rearrange("(p i) r -> p i r", i=PACK)

        def load_words(a):
            nc.sync.dma_start(
                table_words[a][:], tab_words[a].rearrange("p t i -> p (t i)").bitcast(I32)
            )

        nc.vector.memset(table_scales[32:64, :], 0)
        for a in range(PASSES):
            nc.vector.memset(v_planes[a][:], 0)
        nc.gpsimd.memset(wa_plane[:], 0)
        nc.gpsimd.memset(table_scales[64:, :], 0)
        nc.gpsimd.memset(wo_planes[0][:], 0)

        nc.sync.dma_start(
            table_scales[:32, :], tab_scales.rearrange("a q t -> (a q) t").bitcast(I32)
        )
        nc.sync.dma_start(atoms[:], offs)
        for r in range(4):
            nc.sync.dma_start(
                wa_plane[r:P:32, :, :],
                wa_scales[:, r:16:4, :].rearrange("a q c -> q a c").bitcast(I32),
            )
        nc.sync.dma_start(wa_codes[:], wa_words.rearrange("a p b -> p a b").bitcast(I32))
        load_words(0)
        nc.sync.dma_start(wg_pair[:], wg_rows(0)[:, :, : 2 * P])
        nc.sync.dma_start(wg_second[0][:], wg_rows(1)[:, :, :P])
        v_codes, v_plane = {}, {}

        picked_scales = keep.tile([P, S // 4], I32, name="picked_scales")
        nc.vector.tensor_copy(
            picked_scales[:].bitcast(U8), table_scales[:].bitcast(U8).indirect(atoms[:])
        )
        moves = [(a, r) for a in range(PASSES) for r in range(4)]

        def move_scales(a, r):
            nc.sync.dma_start(v_planes[a][r:P:32, :], picked_scales[16 * a + r : 16 * (a + 1) : 4, :])

        for a, r in moves[:4]:
            move_scales(a, r)
        load_words(1)
        for a, r in moves[4:]:
            move_scales(a, r)
        for a in range(PASSES):
            for h in range(HALVES):
                v_plane[a, h] = v_planes[a][:].bitcast(U8)[:, h * BANK : (h + 1) * BANK]
        nc.sync.dma_start(weights[0][:], wgs[:, :BANK])
        nc.sync.dma_start(places[:], offs2)
        nc.sync.dma_start(wg_second[1][:], wg_rows(1)[:, :, P : 2 * P])
        nc.sync.dma_start(weights[1][:], wgs[:, BANK:])
        for i, a in wg_rest:
            nc.sync.dma_start(wg_rest[i, a][:], wg_rows(a)[:, :, i * P : (i + 1) * P])
        nc.sync.dma_start(states[0][:], sites[:P, :])
        nc.sync.dma_start(wo_raw[:], wo.rearrange("(p i) n -> p i n", i=PACK))
        for i in range(1, ROWS):
            nc.sync.dma_start(states[i][:], sites[i * P : (i + 1) * P, :])

        make_identity(nc, identity[:])
        for page in page_tiles:
            for g in range(GROUPS):
                nc.vector.memset(page[:, g * BANK : (g + 1) * BANK].bitcast(I32), 0)

        def gather_words(a, h, picked, pieces=1):
            v_codes[a, h] = picked[:, a, h * BANK : (h + 1) * BANK]
            width = BANK // pieces
            for first in range(h * BANK, (h + 1) * BANK, width):
                nc.vector.tensor_copy(
                    picked[:, a, first : first + width],
                    table_words[a][:].bitcast(U32).indirect(atoms[:, first // 16 : (first + width) // 16]),
                )

        def quantize(grouped, width, name, tag=None):
            codes = keep.tile(
                [P, width], U32, name=f"{name}_codes", tag=tag or f"{name}_codes", align_bytes=64
            )
            plane = keep.tile([P, width], U8, name=f"{name}_plane", align_bytes=64)
            nc.vector.quantize_mx(out=codes[:].bitcast(FP8X4), scales=plane[:], in_=grouped)
            return codes, plane

        wg_q = {}

        def quantize_wg(keys, raws):
            name = "wg" + "".join(f"{i}{a}" for i, a in keys)
            grouped = keep.tile([P, len(keys) * P, PACK], BF16, name=f"{name}_grouped", align_bytes=64)
            width = len(keys) * P // len(raws)
            for n, raw in enumerate(raws):
                nc.scalar.copy(grouped[:, n * width : (n + 1) * width, :], raw[:].rearrange("p i r -> p r i"))
            codes, plane = quantize(grouped[:].rearrange("p r i -> p (r i)"), len(keys) * P, name)
            for n, key in enumerate(keys):
                wg_q[key] = (codes[:, n * P : (n + 1) * P], plane[:, n * P : (n + 1) * P])

        def next_wg(i):
            quantize_wg([(i, a) for a in range(PASSES)], [wg_rest[i, a] for a in range(PASSES)])

        picked = keep.tile([P, PASSES, S], U32, name="picked", align_bytes=64)
        for h in range(HALVES):
            gather_words(0, h, picked)
        quantize_wg([(0, 0), (1, 0)], [wg_pair])
        quantize_wg([(0, 1)], [wg_second[0]])
        gather_words(1, 0, picked, pieces=2)
        gather_words(1, 1, picked)

        product_banks = banks[:4]
        sum_banks = banks[4:]
        messages = {}

        def own_banks(i, h):
            if (i, h) == (ROWS - 1, HALVES - 1):
                return sum_banks[0], sum_banks[1]
            own = sum_banks if i == 1 else product_banks
            return own[2 * h], own[2 * h + 1]

        def gate_pass(i, h, a):
            wg_codes, wg_plane = wg_q[i, a]
            nc.tensor.matmul_mx(
                out=own_banks(i, h)[1][:],
                lhsT=wg_codes.bitcast(FP8X4),
                lhsT_scale=wg_plane,
                rhs=v_codes[a, h].bitcast(FP8X4),
                rhs_scale=v_plane[a, h],
                start=(a == 0),
                stop=(a == PASSES - 1),
            )

        def message_pass(i, h, a):
            nc.tensor.matmul_mx(
                out=own_banks(i, h)[0][:],
                lhsT=wa_codes[:, a, :].bitcast(U8)[:, 2 * i * P : 2 * (i + 1) * P].bitcast(FP4X4),
                lhsT_scale=wa_plane[:, a, :].bitcast(U8)[:, i * P : (i + 1) * P],
                rhs=v_codes[a, h].bitcast(FP8X4),
                rhs_scale=v_plane[a, h],
                start=(a == 0),
                stop=(a == PASSES - 1),
            )

        def new_message(i, h):
            messages[i, h] = keep.tile(
                [P, BANK], F32, name=f"message{i}{h}", tag=f"message{i}{h}", align_bytes=64
            )
            return messages[i, h][:]

        def gate_of(i, h, pieces):
            square = ring.tile([P, BANK], F32, name="square", bufs=2)
            gate = ring.tile([P, BANK], F32, name="gate", bufs=4)
            for cols in pieces:
                nc.scalar.activation(square[:, cols], own_banks(i, h)[1][:, cols], ACT.Square)
                nc.scalar.activation(gate[:, cols], square[:, cols], ACT.Exp, scale=-1.0)
            return gate

        def products(i, h, passes=range(PASSES)):
            for a in passes:
                message_pass(i, h, a)
            raw = ring.tile([P, BANK], F32, name="raw", bufs=4)
            nc.scalar.copy(raw[:], own_banks(i, h)[0][:])
            factor = ring.tile([P, BANK], F32, name="factor", bufs=2)
            nc.gpsimd.tensor_tensor(factor[:], raw[:], weights[h][:], MULT)
            for a in passes:
                gate_pass(i, h, a)
            gate = gate_of(i, h, [slice(0, BANK)])
            nc.gpsimd.tensor_tensor(new_message(i, h), factor[:], gate[:], MULT)

        def last_products():
            i, h = ROWS - 1, HALVES - 1
            for a in range(PASSES):
                message_pass(i, h, a)
            raw = ring.tile([P, BANK], F32, name="raw", bufs=4)
            nc.scalar.copy(raw[:], own_banks(i, h)[0][:])
            for a in range(PASSES):
                gate_pass(i, h, a)
            gate = gate_of(i, h, [slice(0, BANK)])
            nc.gpsimd.tensor_tensor(new_message(i, h), raw[:], gate[:], MULT)

        def last_scatter():
            i, h = ROWS - 1, HALVES - 1
            nc.vector.tensor_tensor(
                pages[i][:].indirect(places[:, h * COLS : (h + 1) * COLS]),
                messages[i, h][:],
                weights[h][:],
                MULT,
            )

        def scatter(i, h, first=0, width=BANK):
            col = h * COLS + first // 16
            nc.vector.tensor_copy(
                pages[i][:].indirect(places[:, col : col + width // 16]),
                messages[i, h][:, first : first + width],
            )

        QUARTER = BANK // 2

        def quarter_passes(q, a):
            cols = slice(q * QUARTER, (q + 1) * QUARTER)
            wg_codes, wg_plane = wg_q[0, a]
            nc.tensor.matmul_mx(
                out=banks[q][:, :QUARTER],
                lhsT=wa_codes[:, a, :].bitcast(U8)[:, : 2 * P].bitcast(FP4X4),
                lhsT_scale=wa_plane[:, a, :].bitcast(U8)[:, :P],
                rhs=v_codes[a, 0][:, cols].bitcast(FP8X4),
                rhs_scale=v_plane[a, 0][:, cols],
                start=(a == 0),
                stop=False,
            )
            nc.tensor.matmul_mx(
                out=banks[q][:, QUARTER:],
                lhsT=wg_codes.bitcast(FP8X4),
                lhsT_scale=wg_plane,
                rhs=v_codes[a, 0][:, cols].bitcast(FP8X4),
                rhs_scale=v_plane[a, 0][:, cols],
                start=False,
                stop=(a == PASSES - 1),
            )

        def first_products():
            message = new_message(0, 0)
            for q in range(2):
                cols = slice(q * QUARTER, (q + 1) * QUARTER)
                quarter_passes(q, 1)
                raw, square, gate, factor = [
                    keep.tile([P, QUARTER], F32, name=f"first_{name}{q}")
                    for name in ("raw", "square", "gate", "factor")
                ]
                nc.scalar.copy(raw[:], banks[q][:, :QUARTER])
                nc.gpsimd.tensor_tensor(factor[:], raw[:], weights[0][:, cols], MULT)
                nc.scalar.activation(square[:], banks[q][:, QUARTER:], ACT.Square)
                nc.scalar.activation(gate[:], square[:], ACT.Exp, scale=-1.0)
                engine = nc.gpsimd if q else nc.vector
                engine.tensor_tensor(message[:, cols], factor[:], gate[:], MULT)
                scatter(0, 0, q * QUARTER, QUARTER)

        def turn(source, first, bank, g):
            for c in range(CHUNKS):
                t0 = g * BANK + c * P
                nc.tensor.matmul(
                    bank[:, c * P : (c + 1) * P],
                    lhsT=source[:, t0 : t0 + P],
                    rhs=identity[:],
                    is_transpose=True,
                    start=(first and c == 0),
                    stop=(not first and c == CHUNKS - 1),
                )

        z_rows = {
            (s, j): keep.tile(
                [P, 2, CHUNKS, 2 * P],
                BF16,
                name=f"z_rows{s}{j}",
                tag=f"table_words{j}" if s == 0 else f"z_rows{j}",
            )
            for s in range(2)
            for j in range(2)
        }

        def copy_on(engine, dst, src):
            if engine == "vector":
                nc.vector.tensor_copy(dst, src)
            else:
                nc.scalar.copy(dst, src)

        def round_z(i, g, engine, into):
            at = P * ((g % 2) ^ (i // 2)) + 64 * (i % 2)
            copy_on(
                engine,
                z_rows[i // 2, g // 2][:, :, :, at : at + 64].rearrange("p u c (m e) -> p u c m e", e=2),
                into[g][:].rearrange("p (c m u e) -> p u c m e", c=CHUNKS, u=2, e=2),
            )

        last = ROWS - 1
        freed_banks = [banks[1], banks[0], banks[3], banks[2]]

        def sums_of(i):
            return freed_banks if i == 2 else sum_banks

        def turn_sites(i, g):
            turn(states[i][:], True, sums_of(i)[g], g)

        def turn_page(i, g, engine="scalar"):
            turn(pages[i][:], False, sums_of(i)[g], g)
            round_z(i, g, engine, sums_of(i))

        z_grouped = [
            keep.tile([P, BANK, PACK], BF16, name=f"z_grouped{g}", tag=f"spent{g}", align_bytes=64)
            for g in range(GROUPS)
        ]

        def turn_back(s, j, half, bank):
            words = z_rows[s, j][:].bitcast(F32)
            for c2 in range(2):
                for u in range(2):
                    col = (2 * c2 + u) * P
                    nc.tensor.transpose(
                        bank[:, col : col + P], words[:, u, 2 * half + c2, :], identity[:]
                    )

        def weave(s, g, half, bank, engine):
            rows = slice(64 * ((g % 2) ^ s), 64 * ((g % 2) ^ s) + 64)
            grouped_words = z_grouped[g][:].rearrange("p t i -> p (t i)").bitcast(F32)
            copy_on(
                engine,
                grouped_words[rows, half * BANK : (half + 1) * BANK].rearrange(
                    "p (c t u) -> p c t u", c=2, u=2
                ),
                bank[rows, :].rearrange("p (c u t) -> p c t u", c=2, u=2),
            )

        for q in range(2):
            quarter_passes(q, 0)
        for i, h in ((0, 1), (1, 0), (1, 1)):
            gate_pass(i, h, 0)
            message_pass(i, h, 0)
        first_products()
        quantize_wg([(1, 1)], [wg_second[1]])
        products(0, 1, [1])
        scatter(0, 1)
        next_wg(2)
        products(1, 0, [1])
        scatter(1, 0)
        next_wg(3)
        products(1, 1, [1])
        scatter(1, 1)
        for h in range(HALVES):
            products(2, h)
        for g in range(GROUPS):
            turn_sites(0, g)
        for g in range(GROUPS):
            turn_page(0, g)
        scatter(2, 0)
        products(last, 0)
        scatter(2, 1)
        for g in range(GROUPS):
            turn_sites(1, g)
        for g in range(2):
            turn_page(1, g)
        last_products()
        for g in range(2, GROUPS):
            turn_page(1, g)
        for g in range(GROUPS):
            turn_sites(2, g)
        scatter(last, 0)
        wo_grouped = keep.tile([P, N, PACK], BF16, name="wo_grouped", align_bytes=64)
        nc.scalar.copy(wo_grouped[:], wo_raw[:].rearrange("p i n -> p n i"))
        for j in range(2):
            for half in range(2):
                bank = sum_banks[2 * j + half]
                turn_back(0, j, half, bank)
                for g in (2 * j, 2 * j + 1):
                    weave(0, g, half, bank, "scalar")
        for g in range(GROUPS):
            turn_page(last - 1, g)
        wo_codes = [
            keep.tile([P, N], U32, name="wo_codes0", tag=f"message{last}0", align_bytes=64),
            keep.tile([P, N], U32, name="wo_codes1", align_bytes=64),
        ]
        nc.vector.quantize_mx(
            out=wo_codes[0][:].bitcast(FP8X4),
            scales=wo_planes[0][:].bitcast(U8),
            in_=wo_grouped[:].rearrange("p n i -> p (n i)"),
        )
        for low in (0, 64):
            there, here = slice(low, low + 64), slice(64 - low, P - low)
            nc.sync.dma_start(wo_codes[1][there, :].bitcast(I32), wo_codes[0][here, :].bitcast(I32))
            nc.sync.dma_start(wo_planes[1][there, :], wo_planes[0][here, :])
        for bank in sum_banks:
            nc.tensor.matmul_mx(
                out=bank[:],
                lhsT=wo_codes[0][:, :P].bitcast(FP8X4),
                lhsT_scale=wo_planes[0][:].bitcast(U8)[:, :P],
                rhs=v_codes[0, 0].bitcast(FP8X4),
                rhs_scale=v_plane[0, 0],
                start=True,
                stop=True,
            )
        last_scatter()
        for g in range(GROUPS):
            turn_sites(last, g)

        out_banks = sum_banks + freed_banks
        z_q = {}

        def quantize_z(g):
            z_q[g] = quantize(z_grouped[g][:].rearrange("p t i -> p (t i)"), BANK, f"z{g}")

        def project(g):
            z_codes, z_plane = z_q[g]
            for n in range(N // P):
                nc.tensor.matmul_mx(
                    out=out_banks[2 * g + n][:],
                    lhsT=wo_codes[g % 2][:, n * P : (n + 1) * P].bitcast(FP8X4),
                    lhsT_scale=wo_planes[g % 2][:].bitcast(U8)[:, n * P : (n + 1) * P],
                    rhs=z_codes[:].bitcast(FP8X4),
                    rhs_scale=z_plane[:],
                    start=True,
                    stop=True,
                )

        def store(g, n, engine):
            result = keep.tile(
                [P, BANK], F32, name=f"result{g}{n}", tag=f"message{g}{n}" if g < last else f"result{n}", align_bytes=64
            )
            copy_on(engine, result[:], out_banks[2 * g + n][:])
            nc.sync.dma_start(out[n * P : (n + 1) * P, g * BANK : (g + 1) * BANK], result[:])

        for g in range(GROUPS):
            turn_page(last, g, "scalar" if g % 2 else "vector")
        for j in range(2):
            for half in range(2):
                turn_back(1, j, half, freed_banks[2 * j + half])
        for g in range(2):
            weave(1, g, 0, freed_banks[0], "vector")
            weave(1, g, 1, freed_banks[1], "scalar")
        for half in range(2):
            weave(1, 2, half, freed_banks[2 + half], "scalar")
        for g in range(2):
            quantize_z(g)
            project(g)
        weave(1, last, 0, freed_banks[2], "vector")
        quantize_z(2)
        weave(1, last, 1, freed_banks[3], "vector")
        project(2)
        for g in range(2):
            for n in range(N // P):
                store(g, n, "scalar")
        quantize_z(last)
        project(last)
        store(2, 0, "scalar")
        store(2, 1, "vector")
        store(last, 0, "vector")
        store(last, 1, "scalar")
